import numpy as np
import ml_dtypes


def mxq(x, axis, fmt="e4m3"):
    dtype, down = {"e4m3": (ml_dtypes.float8_e4m3fn, 7), "e5m2": (ml_dtypes.float8_e5m2, 14)}[fmt]
    v = np.moveaxis(np.asarray(x, np.float32).astype(ml_dtypes.bfloat16).astype(np.float64), axis, -1)
    blocks = v.reshape(v.shape[:-1] + (-1, 32))
    amax = np.abs(blocks).max(-1, keepdims=True)
    byte = np.maximum(np.where(amax > 0, np.frexp(amax)[1] - 1 + 127, 0) - down, 1)
    scale = np.exp2(byte - 127.0)
    codes = (blocks / scale).astype(np.float32).astype(dtype).astype(np.float64)
    return np.moveaxis((codes * scale).reshape(v.shape), -1, axis)


WIDE = False


def mx_kscale(k):
    if not WIDE:
        return np.ones(k)
    levels = np.array([24, -24, 12, -12, 0])
    if k % 512:
        return np.exp2(np.random.permutation(np.resize(levels, k // 32))).repeat(32)
    a = np.empty((k // 512, 16))
    for p in range(k // 512):
        a[p, :8] = np.random.permutation(np.resize(levels, 8))
        for g in range(8):
            far = levels[np.abs(levels - a[p, g]) >= 10]
            a[p, g + 8] = far[np.random.randint(len(far))]
    return np.exp2(a.ravel()).repeat(32)


def f64(x):
    return np.asarray(x).astype(np.float64)


def striped(idx):
    return np.tile(idx.reshape(-1, 16).T, (8, 1)).astype(np.uint16)


def unstriped(offs):
    return offs[:16].T.reshape(-1).astype(np.int64)


E2M1 = np.array([0.0, 0.5, 1.0, 1.5, 2.0, 3.0, 4.0, 6.0, -0.0, -0.5, -1.0, -1.5, -2.0, -3.0, -4.0, -6.0])


def pack_weight(w, fmt):
    k, n = w.shape
    w = f64(np.asarray(w, np.float32).astype(ml_dtypes.bfloat16)).reshape(k // 32, 32, n)
    amax = np.abs(w).max(1)
    if fmt == "e4m3":
        byte = np.frexp(amax)[1] - 1 + 127 - 7
    else:
        mant, ex = np.frexp(amax / 6.0)
        byte = np.where(mant > 0.5, ex, ex - 1) + 127
    byte = np.clip(np.where(amax > 0, byte, 1), 1, 254)
    scaled = (w * np.exp2(127.0 - byte)[:, None, :]).reshape(k, n).astype(np.float32)
    by_word = np.ascontiguousarray(scaled.reshape(k // 512, 128, 4, n).transpose(0, 1, 3, 2))
    if fmt == "e4m3":
        words = by_word.astype(ml_dtypes.float8_e4m3fn).view(np.uint8)
    else:
        c = by_word.astype(ml_dtypes.float4_e2m1fn).view(np.uint8) & 0xF
        words = (c[..., 0::2] | (c[..., 1::2] << 4)).reshape(k // 512, 128, 2 * n)
    return np.ascontiguousarray(words), np.ascontiguousarray(byte.astype(np.uint8).reshape(k // 512, 16, n))


def unpack_weight(words, scales, fmt):
    g, _, n = scales.shape
    words = np.ascontiguousarray(words).reshape(g, 128, n, -1)
    if fmt == "e4m3":
        vals = words.view(ml_dtypes.float8_e4m3fn).astype(np.float64)
    else:
        nib = np.empty((g, 128, n, 4), np.uint8)
        nib[..., 0::2] = words & 0xF
        nib[..., 1::2] = words >> 4
        vals = E2M1[nib]
    vals = vals * np.repeat(np.exp2(scales.astype(np.float64) - 127.0), 8, axis=1)[..., None]
    return vals.transpose(0, 1, 3, 2).reshape(g * 512, n)


K, R, N, T, J = 1024, 512, 512, 2048, 1024


def setup_inputs():
    n = np.random.standard_normal
    s = mx_kscale(K)[:, None]
    u = mx_kscale(R)[:, None]
    p_tab = pack_weight(n((K, T)) * s, "e4m3")
    p_wu = pack_weight(n((K, R)) / np.sqrt(K) / s * u.T, "e2m1")
    p_wd = pack_weight(n((R, N)) / np.sqrt(R) / u, "e4m3")
    return {
        "tab_words": p_tab[0],
        "tab_scales": p_tab[1],
        "wu_words": p_wu[0],
        "wu_scales": p_wu[1],
        "wd_words": p_wd[0],
        "wd_scales": p_wd[1],
        "rT": (n((N, T))).astype(np.float32),
        "b": (0.3 * n(N)).astype(np.float32),
        "wgo": np.tile(np.random.uniform(0.5, 2.0, J), (128, 1)).astype(np.float32),
        "offs": striped(np.random.permutation(T)[:J]),
    }


def reference(tab_words, tab_scales, wu_words, wu_scales, wd_words, wd_scales, rT, b, wgo, offs):
    idx = unstriped(offs)
    tab_ = unpack_weight(tab_words, tab_scales, "e4m3")[:, idx]
    wu_ = unpack_weight(wu_words, wu_scales, "e2m1")
    a = wu_.T @ tab_
    h = np.maximum(a, 0.0)
    h_ = mxq(h, 0, "e4m3")
    wd_ = unpack_weight(wd_words, wd_scales, "e4m3")
    y = wd_.T @ h_
    out = np.zeros((N, T))
    out[:, idx] = f64(wgo)[0] * (y + f64(rT)[:, idx] + f64(b)[:, None])
    return out

@@ -1,0 +1,167 @@
+from contextlib import ExitStack
+
+import concourse.mybir as mybir
+from concourse.masks import make_identity
+
+K, R, N, T, J = 1024, 512, 512, 2048, 1024
+FLOPS = 2 * K * R * J + 2 * R * N * J
+
+F32 = mybir.dt.float32
+BF16 = mybir.dt.bfloat16
+I32 = mybir.dt.int32
+U32 = mybir.dt.uint32
+U16 = mybir.dt.uint16
+U8 = mybir.dt.uint8
+FP8X4 = mybir.dt.float8_e4m3fn_x4
+FP4X4 = mybir.dt.float4_e2m1fn_x4
+ACT = mybir.ActivationFunctionType
+MULT = mybir.AluOpType.mult
+
+P = 128
+HALF = J // 2
+
+
+def tile_list_modp_relu_resb_kernel(tc, tab_words, tab_scales, wu_words, wu_scales, wd_words, wd_scales, rT, b, wgo, offs, out):
+    nc = tc.nc
+    with ExitStack() as ctx:
+        keep = ctx.enter_context(tc.tile_pool(name="keep", bufs=1))
+        ring = ctx.enter_context(tc.tile_pool(name="ring", bufs=2))
+        ps2 = ctx.enter_context(tc.psum_pool(name="ps2", bufs=2))
+        ps1 = ctx.enter_context(tc.psum_pool(name="ps1", bufs=1))
+
+        offsets = keep.tile([P, J // 16], U16, name="offsets")
+        nc.sync.dma_start(offsets[:], offs)
+
+        tabs = keep.tile([P, T], U8, name="tabs", align_bytes=64)
+        nc.vector.memset(tabs[:].bitcast(I32), 0)
+        for q in range(4):
+            nc.scalar.dma_start(tabs[32 * q : 32 * q + 8, :].bitcast(I32), tab_scales[:, 4 * q : 4 * q + 4, :].bitcast(I32))
+        tabw = []
+        for a in range(2):
+            w = keep.tile([P, T], I32, name="tabw%d" % a, align_bytes=64)
+            nc.sync.dma_start(w[:], tab_words[a].rearrange("p t i -> p (t i)").bitcast(I32))
+            tabw.append(w)
+
+        wu = keep.tile([P, 2, 2 * R], U8, name="wu", align_bytes=64)
+        nc.sync.dma_start(wu[:].bitcast(I32), wu_words.rearrange("a p n -> p a n").bitcast(I32))
+        wus = keep.tile([P, 2, R], U8, name="wus", align_bytes=64)
+        nc.vector.memset(wus[:].bitcast(I32), 0)
+        for q in range(4):
+            nc.sync.dma_start(wus[32 * q : 32 * q + 4, :, :].bitcast(I32), wu_scales[:, 4 * q : 4 * q + 4, :].rearrange("a r n -> r a n").bitcast(I32))
+        plane1 = keep.tile([P, J], U8, name="plane1", align_bytes=64)
+        nc.vector.memset(plane1[:].bitcast(I32), 0)
+        wds = keep.tile([P, N], U8, name="wds", align_bytes=64)
+        nc.vector.memset(wds[:].bitcast(I32), 0)
+
+        pages = []
+        for i in range(2):
+            page = keep.tile([P, T], F32, name="page%d" % i, align_bytes=64)
+            nc.vector.memset(page[:], 0.0)
+            pages.append(page)
+
+        ident = keep.tile([P, P], F32, name="ident", align_bytes=64)
+        make_identity(nc, ident[:])
+
+        r_rows = rT.rearrange("(p c) t -> p c t", c=4)
+        out_rows = out.rearrange("(p c) t -> p c t", c=4)
+        res = []
+        for c in range(4):
+            rt = keep.tile([P, T], F32, name="res%d" % c, align_bytes=64)
+            res.append(rt)
+        nc.sync.dma_start(res[0][:], r_rows[:, 0, :])
+        wd = keep.tile([P, N], I32, name="wd", align_bytes=64)
+        nc.sync.dma_start(wd[:], wd_words[0].rearrange("p n i -> p (n i)").bitcast(I32))
+        for q in range(4):
+            nc.sync.dma_start(wds[32 * q : 32 * q + 4, :].bitcast(I32), wd_scales[0, 4 * q : 4 * q + 4, :].bitcast(I32))
+        nc.sync.dma_start(res[1][:], r_rows[:, 1, :])
+        bias = keep.tile([P, 4], F32, name="bias")
+        nc.sync.dma_start(bias[:], b.rearrange("(p c) -> p c", c=4))
+        nc.sync.dma_start(res[2][:], r_rows[:, 2, :])
+        nc.sync.dma_start(res[3][:], r_rows[:, 3, :])
+        gate = keep.tile([P, J], F32, name="gate", align_bytes=64)
+        nc.sync.dma_start(gate[:], wgo)
+
+        plane0 = keep.tile([P, J], U8, name="plane0", align_bytes=64)
+        nc.vector.tensor_copy(plane0[:], tabs[:].indirect(offsets[:]))
+        nc.scalar.dma_start(plane1[0:112, :].bitcast(I32), plane0[4:116, :].bitcast(I32))
+        planes = [plane0, plane1]
+        words0 = keep.tile([P, J], U32, name="words0", align_bytes=64)
+        nc.vector.tensor_copy(words0[:], tabw[0][:].bitcast(U32).indirect(offsets[:]))
+        words1 = []
+        for h in range(2):
+            w = keep.tile([P, HALF], U32, name="words1_%d" % h, align_bytes=64)
+            nc.vector.tensor_copy(w[:], tabw[1][:].bitcast(U32).indirect(offsets[:, 32 * h : 32 * h + 32]))
+            words1.append(w)
+
+        y_sb = []
+
+        def mlp_pair(g):
+            xt = ps1.tile([P, 2, 2, P], F32, name="xt")
+            for i in range(2):
+                j0 = (2 * g + i) * P
+                cols = slice(j0, j0 + P)
+                aT = ps2.tile([P, R], F32, name="aT")
+                nc.tensor.matmul_mx(out=aT[:], lhsT=words0[:, cols].bitcast(FP8X4), lhsT_scale=planes[0][:, cols],
+                                    rhs=wu[:, 0, :].bitcast(FP4X4), rhs_scale=wus[:, 0, :], start=True, stop=False)
+                nc.tensor.matmul_mx(out=aT[:], lhsT=words1[j0 // HALF][:, j0 % HALF : j0 % HALF + P].bitcast(FP8X4), lhsT_scale=planes[1][:, cols],
+                                    rhs=wu[:, 1, :].bitcast(FP4X4), rhs_scale=wus[:, 1, :], start=False, stop=True)
+                hb = ring.tile([P, 2, P, 2], BF16, name="hb", align_bytes=64)
+                nc.scalar.activation(hb[:], aT[:].rearrange("j (p u e) -> j u p e", u=2, e=2), ACT.Relu)
+                hw = hb[:].rearrange("j u p e -> j (u p e)").bitcast(F32)
+                for u in range(2):
+                    nc.tensor.transpose(xt[:, i, u, :], hw[:, u * P : (u + 1) * P], ident[:])
+            hT = ring.tile([P, 2 * P * 4], BF16, name="hT", align_bytes=64)
+            nc.scalar.copy(hT[:].bitcast(F32).rearrange("p (i j u) -> p i j u", i=2, u=2), xt[:].rearrange("p i u j -> p i j u"))
+            hq = ring.tile([P, 2 * P], U32, name="hq", align_bytes=64)
+            hs = ring.tile([P, 2 * P], U8, name="hs", align_bytes=64)
+            nc.vector.quantize_mx(out=hq[:].bitcast(FP8X4), scales=hs[:], in_=hT[:])
+            for i in range(2):
+                yT = ps2.tile([P, N], F32, name="yT")
+                nc.tensor.matmul_mx(out=yT[:], lhsT=hq[:, i * P : (i + 1) * P].bitcast(FP8X4), lhsT_scale=hs[:, i * P : (i + 1) * P],
+                                    rhs=wd[:].bitcast(FP8X4), rhs_scale=wds[:], start=True, stop=True)
+                ys = keep.tile([P, 4, P], F32, name="ys%d" % (2 * g + i), align_bytes=64)
+                nc.scalar.copy(ys[:], yT[:].rearrange("j (m c) -> j c m", c=4))
+                y_sb.append(ys)
+
+        r_sb = {}
+
+        def gather_res(c):
+            rg = keep.tile([P, J], F32, name="rg%d" % c, align_bytes=64)
+            nc.vector.tensor_copy(rg[:], res[c][:].indirect(offsets[:]))
+            for h in range(2):
+                rj = ps1.tile([P, 4, P], F32, name="rj")
+                for i in range(4):
+                    j0 = (4 * h + i) * P
+                    nc.tensor.transpose(rj[:, i, :], rg[:, j0 : j0 + P], ident[:])
+                rs = keep.tile([P, 4, P], F32, name="rs%d_%d" % (c, h), align_bytes=64)
+                nc.scalar.copy(rs[:], rj[:])
+                r_sb[(c, h)] = rs
+
+        def sum_half(c, h, z):
+            zp = ps2.tile([P, 4, P], F32, name="zp")
+            for i in range(4):
+                nc.tensor.matmul(zp[:, i, :], r_sb[(c, h)][:, i, :], ident[:], start=True, stop=False, is_transpose=True)
+                nc.tensor.matmul(zp[:, i, :], y_sb[4 * h + i][:, c, :], ident[:], start=False, stop=True, is_transpose=True)
+            nc.scalar.activation(z[:, h * HALF : (h + 1) * HALF], zp[:].rearrange("m i j -> m (i j)"), ACT.Identity, bias=bias[:, c : c + 1])
+
+        mlp_pair(0)
+        mlp_pair(1)
+        gather_res(0)
+        mlp_pair(2)
+        mlp_pair(3)
+        for c in range(1, 4):
+            gather_res(c)
+
+        for c in range(4):
+            z = keep.tile([P, J], F32, name="z%d" % c, align_bytes=64)
+            page = pages[c % 2]
+            if c == 0:
+                for h in range(2):
+                    sum_half(c, h, z)
+                    cols = slice(h * HALF, (h + 1) * HALF)
+                    nc.vector.tensor_tensor(page[:].indirect(offsets[:, 32 * h : 32 * h + 32]), z[:, cols], gate[:, cols], MULT)
+            else:
+                for h in range(2):
+                    sum_half(c, h, z)
+                nc.vector.tensor_tensor(page[:].indirect(offsets[:]), z[:], gate[:], MULT)
+            nc.sync.dma_start(out_rows[:, c, :], page[:])

@@ -25,82 +25,84 @@ def tile_list_modp_relu_resb_kernel(tc, tab_words, tab_scales, wu_words, wu_scal
     nc = tc.nc
     with ExitStack() as ctx:
         keep = ctx.enter_context(tc.tile_pool(name="keep", bufs=1))
+        reuse = ctx.enter_context(tc.tile_pool(name="reuse", bufs=1))
         ring = ctx.enter_context(tc.tile_pool(name="ring", bufs=2))
-        ps2 = ctx.enter_context(tc.psum_pool(name="ps2", bufs=2))
-        ps1 = ctx.enter_context(tc.psum_pool(name="ps1", bufs=1))
+        psum = ctx.enter_context(tc.psum_pool(name="psum", bufs=1))
+        banks = [psum.tile([P, 512], F32, name="bank%d" % i) for i in range(8)]
 
         offsets = keep.tile([P, J // 16], U16, name="offsets")
         nc.sync.dma_start(offsets[:], offs)
 
-        tabs = keep.tile([P, T], U8, name="tabs", align_bytes=64)
-        nc.vector.memset(tabs[:].bitcast(I32), 0)
-        for q in range(4):
-            nc.scalar.dma_start(tabs[32 * q : 32 * q + 8, :].bitcast(I32), tab_scales[:, 4 * q : 4 * q + 4, :].bitcast(I32))
-        tabw = []
-        for a in range(2):
-            w = keep.tile([P, T], I32, name="tabw%d" % a, align_bytes=64)
-            nc.sync.dma_start(w[:], tab_words[a].rearrange("p t i -> p (t i)").bitcast(I32))
-            tabw.append(w)
-
-        wu = keep.tile([P, 2, 2 * R], U8, name="wu", align_bytes=64)
-        nc.sync.dma_start(wu[:].bitcast(I32), wu_words.rearrange("a p n -> p a n").bitcast(I32))
-        wus = keep.tile([P, 2, R], U8, name="wus", align_bytes=64)
-        nc.vector.memset(wus[:].bitcast(I32), 0)
-        for q in range(4):
-            nc.sync.dma_start(wus[32 * q : 32 * q + 4, :, :].bitcast(I32), wu_scales[:, 4 * q : 4 * q + 4, :].rearrange("a r n -> r a n").bitcast(I32))
-        plane1 = keep.tile([P, J], U8, name="plane1", align_bytes=64)
-        nc.vector.memset(plane1[:].bitcast(I32), 0)
-        wds = keep.tile([P, N], U8, name="wds", align_bytes=64)
-        nc.vector.memset(wds[:].bitcast(I32), 0)
-
-        pages = []
-        for i in range(2):
-            page = keep.tile([P, T], F32, name="page%d" % i, align_bytes=64)
-            nc.vector.memset(page[:], 0.0)
-            pages.append(page)
-
-        ident = keep.tile([P, P], F32, name="ident", align_bytes=64)
-        make_identity(nc, ident[:])
-
         r_rows = rT.rearrange("(p c) t -> p c t", c=4)
         out_rows = out.rearrange("(p c) t -> p c t", c=4)
+
+        tabs = reuse.tile([P, T], U8, name="tabs", align_bytes=64, offset=7168)
+        nc.vector.memset(tabs[:].bitcast(I32), 0)
+        wus = keep.tile([P, 2, R], U8, name="wus", align_bytes=64)
+        nc.vector.memset(wus[:].bitcast(I32), 0)
+        plane1 = keep.tile([P, J], U8, name="plane1", align_bytes=64)
+        nc.vector.memset(plane1[:].bitcast(I32), 0)
+        ident = keep.tile([P, P], F32, name="ident", align_bytes=64)
+        make_identity(nc, ident[:])
+        pages = []
+        for i in range(4):
+            page = keep.tile([P, T], F32, name="page%d" % i, align_bytes=64)
+            nc.gpsimd.memset(page[:], 0.0)
+            pages.append(page)
+
+        wu = keep.tile([P, 2, 2 * R], U8, name="wu", align_bytes=64)
+        tabw = [reuse.tile([P, T], I32, name="tabw%d" % a, align_bytes=64, offset=(10240, 18944)[a]) for a in range(2)]
         res = []
-        for c in range(4):
-            rt = keep.tile([P, T], F32, name="res%d" % c, align_bytes=64)
+
+        def load_res(c):
+            rt = reuse.tile([P, T], F32, name="res%d" % c, align_bytes=64, offset=(0, 10752, 18944, 0)[c])
+            nc.sync.dma_start(rt[:], r_rows[:, c, :])
             res.append(rt)
-        nc.sync.dma_start(res[0][:], r_rows[:, 0, :])
-        wd = keep.tile([P, N], I32, name="wd", align_bytes=64)
-        nc.sync.dma_start(wd[:], wd_words[0].rearrange("p n i -> p (n i)").bitcast(I32))
-        for q in range(4):
-            nc.sync.dma_start(wds[32 * q : 32 * q + 4, :].bitcast(I32), wd_scales[0, 4 * q : 4 * q + 4, :].bitcast(I32))
-        nc.sync.dma_start(res[1][:], r_rows[:, 1, :])
+
         bias = keep.tile([P, 4], F32, name="bias")
+
+        nc.sync.dma_start(wu[:].bitcast(I32), wu_words.rearrange("a p n -> p a n").bitcast(I32))
+        for q in range(4):
+            nc.sync.dma_start(tabs[32 * q : 32 * q + 8, :].bitcast(I32), tab_scales[:, 4 * q : 4 * q + 4, :].bitcast(I32))
+        nc.sync.dma_start(tabw[0][:], tab_words[0].rearrange("p t i -> p (t i)").bitcast(I32))
+        nc.sync.dma_start(tabw[1][:], tab_words[1].rearrange("p t i -> p (t i)").bitcast(I32))
+        for q in range(4):
+            nc.sync.dma_start(wus[32 * q : 32 * q + 4, :, :].bitcast(I32), wu_scales[:, 4 * q : 4 * q + 4, :].rearrange("a r n -> r a n").bitcast(I32))
         nc.sync.dma_start(bias[:], b.rearrange("(p c) -> p c", c=4))
-        nc.sync.dma_start(res[2][:], r_rows[:, 2, :])
-        nc.sync.dma_start(res[3][:], r_rows[:, 3, :])
-        gate = keep.tile([P, J], F32, name="gate", align_bytes=64)
-        nc.sync.dma_start(gate[:], wgo)
 
         plane0 = keep.tile([P, J], U8, name="plane0", align_bytes=64)
         nc.vector.tensor_copy(plane0[:], tabs[:].indirect(offsets[:]))
         nc.scalar.dma_start(plane1[0:112, :].bitcast(I32), plane0[4:116, :].bitcast(I32))
         planes = [plane0, plane1]
+        load_res(0)
+        wd = reuse.tile([P, N], I32, name="wd", align_bytes=64, offset=8192)
+        nc.sync.dma_start(wd[:], wd_words[0].rearrange("p n i -> p (n i)").bitcast(I32))
+
         words0 = keep.tile([P, J], U32, name="words0", align_bytes=64)
         nc.vector.tensor_copy(words0[:], tabw[0][:].bitcast(U32).indirect(offsets[:]))
+        load_res(1)
+        wds = reuse.tile([P, N], U8, name="wds", align_bytes=64, offset=10240)
+        nc.vector.memset(wds[:].bitcast(I32), 0)
+        for q in range(4):
+            nc.sync.dma_start(wds[32 * q : 32 * q + 4, :].bitcast(I32), wd_scales[0, 4 * q : 4 * q + 4, :].bitcast(I32))
         words1 = []
         for h in range(2):
             w = keep.tile([P, HALF], U32, name="words1_%d" % h, align_bytes=64)
             nc.vector.tensor_copy(w[:], tabw[1][:].bitcast(U32).indirect(offsets[:, 32 * h : 32 * h + 32]))
             words1.append(w)
+        load_res(2)
 
-        y_sb = []
+        h_t = [keep.tile([P, HALF * 4], BF16, name="hT%d" % h, align_bytes=64) for h in range(2)]
+        y_sb = [keep.tile([P, 4, P], F32, name="ys%d" % i, align_bytes=64) for i in range(8)]
+        zs = [keep.tile([P, J], F32, name="z%d" % c, align_bytes=64) for c in range(4)]
+        r_g = [keep.tile([P, J], F32, name="rg%d" % c, align_bytes=64) for c in range(4)]
 
-        def mlp_pair(g):
-            xt = ps1.tile([P, 2, 2, P], F32, name="xt")
+        def up_pair(g, a_banks, x_bank):
+            xt = x_bank[:].rearrange("p (i u j) -> p i u j", i=2, u=2)
             for i in range(2):
                 j0 = (2 * g + i) * P
                 cols = slice(j0, j0 + P)
-                aT = ps2.tile([P, R], F32, name="aT")
+                aT = a_banks[i]
                 nc.tensor.matmul_mx(out=aT[:], lhsT=words0[:, cols].bitcast(FP8X4), lhsT_scale=planes[0][:, cols],
                                     rhs=wu[:, 0, :].bitcast(FP4X4), rhs_scale=wus[:, 0, :], start=True, stop=False)
                 nc.tensor.matmul_mx(out=aT[:], lhsT=words1[j0 // HALF][:, j0 % HALF : j0 % HALF + P].bitcast(FP8X4), lhsT_scale=planes[1][:, cols],
@@ -110,58 +112,62 @@ def tile_list_modp_relu_resb_kernel(tc, tab_words, tab_scales, wu_words, wu_scal
                 hw = hb[:].rearrange("j u p e -> j (u p e)").bitcast(F32)
                 for u in range(2):
                     nc.tensor.transpose(xt[:, i, u, :], hw[:, u * P : (u + 1) * P], ident[:])
-            hT = ring.tile([P, 2 * P * 4], BF16, name="hT", align_bytes=64)
-            nc.scalar.copy(hT[:].bitcast(F32).rearrange("p (i j u) -> p i j u", i=2, u=2), xt[:].rearrange("p i u j -> p i j u"))
-            hq = ring.tile([P, 2 * P], U32, name="hq", align_bytes=64)
-            hs = ring.tile([P, 2 * P], U8, name="hs", align_bytes=64)
-            nc.vector.quantize_mx(out=hq[:].bitcast(FP8X4), scales=hs[:], in_=hT[:])
-            for i in range(2):
-                yT = ps2.tile([P, N], F32, name="yT")
+            dst = h_t[g // 2][:].bitcast(F32)[:, (g % 2) * 4 * P : (g % 2 + 1) * 4 * P]
+            nc.scalar.copy(dst.rearrange("p (i j u) -> p i j u", i=2, u=2), xt.rearrange("p i u j -> p i j u"))
+
+        def down_half(h, y_banks):
+            hq = ring.tile([P, HALF], U32, name="hq", align_bytes=64)
+            hs = ring.tile([P, HALF], U8, name="hs", align_bytes=64)
+            nc.vector.quantize_mx(out=hq[:].bitcast(FP8X4), scales=hs[:], in_=h_t[h][:])
+            for i in range(4):
+                yT = y_banks[i % 2]
                 nc.tensor.matmul_mx(out=yT[:], lhsT=hq[:, i * P : (i + 1) * P].bitcast(FP8X4), lhsT_scale=hs[:, i * P : (i + 1) * P],
                                     rhs=wd[:].bitcast(FP8X4), rhs_scale=wds[:], start=True, stop=True)
-                ys = keep.tile([P, 4, P], F32, name="ys%d" % (2 * g + i), align_bytes=64)
-                nc.scalar.copy(ys[:], yT[:].rearrange("j (m c) -> j c m", c=4))
-                y_sb.append(ys)
-
-        r_sb = {}
+                nc.scalar.copy(y_sb[4 * h + i][:], yT[:].rearrange("j (m c) -> j c m", c=4))
 
         def gather_res(c):
-            rg = keep.tile([P, J], F32, name="rg%d" % c, align_bytes=64)
-            nc.vector.tensor_copy(rg[:], res[c][:].indirect(offsets[:]))
-            for h in range(2):
-                rj = ps1.tile([P, 4, P], F32, name="rj")
-                for i in range(4):
-                    j0 = (4 * h + i) * P
-                    nc.tensor.transpose(rj[:, i, :], rg[:, j0 : j0 + P], ident[:])
-                rs = keep.tile([P, 4, P], F32, name="rs%d_%d" % (c, h), align_bytes=64)
-                nc.scalar.copy(rs[:], rj[:])
-                r_sb[(c, h)] = rs
+            nc.vector.tensor_copy(r_g[c][:], res[c][:].indirect(offsets[:]))
 
-        def sum_half(c, h, z):
-            zp = ps2.tile([P, 4, P], F32, name="zp")
+        def sum_half(c, h):
+            rj = banks[5][:].rearrange("j (i m) -> j i m", i=4)
             for i in range(4):
-                nc.tensor.matmul(zp[:, i, :], r_sb[(c, h)][:, i, :], ident[:], start=True, stop=False, is_transpose=True)
-                nc.tensor.matmul(zp[:, i, :], y_sb[4 * h + i][:, c, :], ident[:], start=False, stop=True, is_transpose=True)
-            nc.scalar.activation(z[:, h * HALF : (h + 1) * HALF], zp[:].rearrange("m i j -> m (i j)"), ACT.Identity, bias=bias[:, c : c + 1])
+                j0 = (4 * h + i) * P
+                nc.tensor.transpose(rj[:, i, :], r_g[c][:, j0 : j0 + P], ident[:])
+            rs = ring.tile([P, 4, P], F32, name="rs", align_bytes=64)
+            nc.scalar.copy(rs[:], rj)
+            zp = banks[6 + c % 2]
+            for i in range(4):
+                nc.tensor.matmul(zp[:, i * P : (i + 1) * P], rs[:, i, :], ident[:], start=True, stop=False, is_transpose=True)
+                nc.tensor.matmul(zp[:, i * P : (i + 1) * P], y_sb[4 * h + i][:, c, :], ident[:], start=False, stop=True, is_transpose=True)
+            nc.scalar.activation(zs[c][:, h * HALF : (h + 1) * HALF], zp[:], ACT.Identity, bias=bias[:, c : c + 1])
 
-        mlp_pair(0)
-        mlp_pair(1)
+        def scatter(c, h):
+            cols = slice(h * HALF, (h + 1) * HALF)
+            nc.vector.tensor_tensor(pages[c][:].indirect(offsets[:, 32 * h : 32 * h + 32]), zs[c][:, cols], gate[:, cols], MULT)
+
+        up_pair(0, banks[0:2], banks[2])
+        up_pair(1, banks[0:2], banks[3])
+
         gather_res(0)
-        mlp_pair(2)
-        mlp_pair(3)
-        for c in range(1, 4):
-            gather_res(c)
+        load_res(3)
+        gather_res(1)
+        gate = reuse.tile([P, J], F32, name="gate", align_bytes=64, offset=10752)
+        nc.sync.dma_start(gate[:], wgo)
+        down_half(0, banks[0:2])
+        gather_res(2)
+        gather_res(3)
+        sum_half(0, 0)
 
+        scatter(0, 0)
+        up_pair(2, banks[2:4], banks[4])
+        sum_half(1, 0)
+        scatter(1, 0)
+        up_pair(3, banks[0:2], banks[2])
+        down_half(1, banks[3:5])
+        for c in range(2, 4):
+            sum_half(c, 0)
+            scatter(c, 0)
         for c in range(4):
-            z = keep.tile([P, J], F32, name="z%d" % c, align_bytes=64)
-            page = pages[c % 2]
-            if c == 0:
-                for h in range(2):
-                    sum_half(c, h, z)
-                    cols = slice(h * HALF, (h + 1) * HALF)
-                    nc.vector.tensor_tensor(page[:].indirect(offsets[:, 32 * h : 32 * h + 32]), z[:, cols], gate[:, cols], MULT)
-            else:
-                for h in range(2):
-                    sum_half(c, h, z)
-                nc.vector.tensor_tensor(page[:].indirect(offsets[:]), z[:], gate[:], MULT)
-            nc.sync.dma_start(out_rows[:, c, :], page[:])
+            sum_half(c, 1)
+            scatter(c, 1)
+            nc.sync.dma_start(out_rows[:, c, :], pages[c][:])

@@ -26,147 +26,150 @@ def tile_list_modp_relu_resb_kernel(tc, tab_words, tab_scales, wu_words, wu_scal
     with ExitStack() as ctx:
         keep = ctx.enter_context(tc.tile_pool(name="keep", bufs=1))
         reuse = ctx.enter_context(tc.tile_pool(name="reuse", bufs=1))
+        picks = ctx.enter_context(tc.tile_pool(name="picks", bufs=1))
         ring = ctx.enter_context(tc.tile_pool(name="ring", bufs=2))
         psum = ctx.enter_context(tc.psum_pool(name="psum", bufs=1))
         banks = [psum.tile([P, 512], F32, name="bank%d" % i) for i in range(8)]
 
         offsets = keep.tile([P, J // 16], U16, name="offsets")
         nc.sync.dma_start(offsets[:], offs)
+        half_offsets = [offsets[:, 32 * h : 32 * h + 32] for h in range(2)]
 
         r_rows = rT.rearrange("(p c) t -> p c t", c=4)
         out_rows = out.rearrange("(p c) t -> p c t", c=4)
 
-        tabs = reuse.tile([P, T], U8, name="tabs", align_bytes=64, offset=7168)
+        tabs = reuse.tile([P, T], U8, name="tabs", align_bytes=64, offset=7680)
         nc.vector.memset(tabs[:].bitcast(I32), 0)
         wus = keep.tile([P, 2, R], U8, name="wus", align_bytes=64)
         nc.vector.memset(wus[:].bitcast(I32), 0)
-        plane1 = keep.tile([P, J], U8, name="plane1", align_bytes=64)
-        nc.vector.memset(plane1[:].bitcast(I32), 0)
+        plane1 = [keep.tile([P, HALF], U8, name="plane1_%d" % h, align_bytes=64) for h in range(2)]
+        for h in range(2):
+            nc.vector.memset(plane1[h][:].bitcast(I32), 0)
         ident = keep.tile([P, P], F32, name="ident", align_bytes=64)
         make_identity(nc, ident[:])
         pages = []
-        for i in range(4):
+        for i in range(2):
             page = keep.tile([P, T], F32, name="page%d" % i, align_bytes=64)
-            nc.gpsimd.memset(page[:], 0.0)
+            nc.vector.memset(page[:], 0.0)
             pages.append(page)
 
         wu = keep.tile([P, 2, 2 * R], U8, name="wu", align_bytes=64)
-        tabw = [reuse.tile([P, T], I32, name="tabw%d" % a, align_bytes=64, offset=(10240, 18944)[a]) for a in range(2)]
+        tabw = [reuse.tile([P, T], I32, name="tabw%d" % a, align_bytes=64, offset=(16960, 31296)[a]) for a in range(2)]
         res = []
 
         def load_res(c):
-            rt = reuse.tile([P, T], F32, name="res%d" % c, align_bytes=64, offset=(0, 10752, 18944, 0)[c])
+            rt = reuse.tile([P, T], F32, name="res%d" % c, align_bytes=64, offset=(0, 8768, 19008, 31296)[c])
             nc.sync.dma_start(rt[:], r_rows[:, c, :])
             res.append(rt)
-
-        bias = keep.tile([P, 4], F32, name="bias")
 
         nc.sync.dma_start(wu[:].bitcast(I32), wu_words.rearrange("a p n -> p a n").bitcast(I32))
         for q in range(4):
             nc.sync.dma_start(tabs[32 * q : 32 * q + 8, :].bitcast(I32), tab_scales[:, 4 * q : 4 * q + 4, :].bitcast(I32))
-        nc.sync.dma_start(tabw[0][:], tab_words[0].rearrange("p t i -> p (t i)").bitcast(I32))
-        nc.sync.dma_start(tabw[1][:], tab_words[1].rearrange("p t i -> p (t i)").bitcast(I32))
+        for a in range(2):
+            nc.sync.dma_start(tabw[a][:], tab_words[a].rearrange("p t i -> p (t i)").bitcast(I32))
         for q in range(4):
             nc.sync.dma_start(wus[32 * q : 32 * q + 4, :, :].bitcast(I32), wu_scales[:, 4 * q : 4 * q + 4, :].rearrange("a r n -> r a n").bitcast(I32))
-        nc.sync.dma_start(bias[:], b.rearrange("(p c) -> p c", c=4))
 
-        plane0 = keep.tile([P, J], U8, name="plane0", align_bytes=64)
-        nc.vector.tensor_copy(plane0[:], tabs[:].indirect(offsets[:]))
-        nc.scalar.dma_start(plane1[0:112, :].bitcast(I32), plane0[4:116, :].bitcast(I32))
+        plane0 = [keep.tile([P, HALF], U8, name="plane0_%d" % h, align_bytes=64) for h in range(2)]
+        for h in range(2):
+            nc.vector.tensor_copy(plane0[h][:], tabs[:].indirect(half_offsets[h]))
+            nc.scalar.dma_start(plane1[h][0:112, :].bitcast(I32), plane0[h][4:116, :].bitcast(I32))
         planes = [plane0, plane1]
         load_res(0)
-        wd = reuse.tile([P, N], I32, name="wd", align_bytes=64, offset=8192)
-        nc.sync.dma_start(wd[:], wd_words[0].rearrange("p n i -> p (n i)").bitcast(I32))
-
-        words0 = keep.tile([P, J], U32, name="words0", align_bytes=64)
-        nc.vector.tensor_copy(words0[:], tabw[0][:].bitcast(U32).indirect(offsets[:]))
         load_res(1)
-        wds = reuse.tile([P, N], U8, name="wds", align_bytes=64, offset=10240)
+        wds = reuse.tile([P, N], U8, name="wds", align_bytes=64, offset=8192)
         nc.vector.memset(wds[:].bitcast(I32), 0)
         for q in range(4):
             nc.sync.dma_start(wds[32 * q : 32 * q + 4, :].bitcast(I32), wd_scales[0, 4 * q : 4 * q + 4, :].bitcast(I32))
-        words1 = []
-        for h in range(2):
-            w = keep.tile([P, HALF], U32, name="words1_%d" % h, align_bytes=64)
-            nc.vector.tensor_copy(w[:], tabw[1][:].bitcast(U32).indirect(offsets[:, 32 * h : 32 * h + 32]))
-            words1.append(w)
-        load_res(2)
 
-        h_t = [keep.tile([P, HALF * 4], BF16, name="hT%d" % h, align_bytes=64) for h in range(2)]
+        words = [[keep.tile([P, HALF], U32, name="words%d_%d" % (a, h), align_bytes=64) for h in range(2)] for a in range(2)]
+        for h in range(2):
+            for a in range(2):
+                nc.vector.tensor_copy(words[a][h][:], tabw[a][:].bitcast(U32).indirect(half_offsets[h]))
+        bias = reuse.tile([P, 4], F32, name="bias", align_bytes=64, offset=8704)
+        nc.sync.dma_start(bias[:], b.rearrange("(p c) -> p c", c=4))
+        wd = reuse.tile([P, N], I32, name="wd", align_bytes=64, offset=16960)
+        nc.sync.dma_start(wd[:], wd_words[0].rearrange("p n i -> p (n i)").bitcast(I32))
+        load_res(2)
+        load_res(3)
+
         y_sb = [keep.tile([P, 4, P], F32, name="ys%d" % i, align_bytes=64) for i in range(8)]
         zs = [keep.tile([P, J], F32, name="z%d" % c, align_bytes=64) for c in range(4)]
-        r_g = [keep.tile([P, J], F32, name="rg%d" % c, align_bytes=64) for c in range(4)]
+        r_g = {}
+        h_t = [picks.tile([P, HALF * 4], BF16, name="hT%d" % h, align_bytes=64, offset=(2048, 16384)[h]) for h in range(2)]
 
-        def up_pair(g, a_banks, x_bank):
-            xt = x_bank[:].rearrange("p (i u j) -> p i u j", i=2, u=2)
+        def up_pair(g):
+            xt = banks[2 + g % 2][:].rearrange("p (i u j) -> p i u j", i=2, u=2)
+            h = g // 2
             for i in range(2):
-                j0 = (2 * g + i) * P
+                j0 = (2 * (g % 2) + i) * P
                 cols = slice(j0, j0 + P)
-                aT = a_banks[i]
-                nc.tensor.matmul_mx(out=aT[:], lhsT=words0[:, cols].bitcast(FP8X4), lhsT_scale=planes[0][:, cols],
-                                    rhs=wu[:, 0, :].bitcast(FP4X4), rhs_scale=wus[:, 0, :], start=True, stop=False)
-                nc.tensor.matmul_mx(out=aT[:], lhsT=words1[j0 // HALF][:, j0 % HALF : j0 % HALF + P].bitcast(FP8X4), lhsT_scale=planes[1][:, cols],
-                                    rhs=wu[:, 1, :].bitcast(FP4X4), rhs_scale=wus[:, 1, :], start=False, stop=True)
+                aT = banks[5 * h + i]
+                for a in range(2):
+                    nc.tensor.matmul_mx(out=aT[:], lhsT=words[a][h][:, cols].bitcast(FP8X4), lhsT_scale=planes[a][h][:, cols],
+                                        rhs=wu[:, a, :].bitcast(FP4X4), rhs_scale=wus[:, a, :], start=(a == 0), stop=(a == 1))
                 hb = ring.tile([P, 2, P, 2], BF16, name="hb", align_bytes=64)
                 nc.scalar.activation(hb[:], aT[:].rearrange("j (p u e) -> j u p e", u=2, e=2), ACT.Relu)
                 hw = hb[:].rearrange("j u p e -> j (u p e)").bitcast(F32)
                 for u in range(2):
                     nc.tensor.transpose(xt[:, i, u, :], hw[:, u * P : (u + 1) * P], ident[:])
-            dst = h_t[g // 2][:].bitcast(F32)[:, (g % 2) * 4 * P : (g % 2 + 1) * 4 * P]
-            nc.scalar.copy(dst.rearrange("p (i j u) -> p i j u", i=2, u=2), xt.rearrange("p i u j -> p i j u"))
+            nc.scalar.copy(h_t[h][:].bitcast(F32)[:, (g % 2) * 4 * P : (g % 2 + 1) * 4 * P].rearrange("p (i j u) -> p i j u", i=2, u=2), xt.rearrange("p i u j -> p i j u"))
 
-        def down_half(h, y_banks):
-            hq = ring.tile([P, HALF], U32, name="hq", align_bytes=64)
+        def down_half(h):
+            hq = reuse.tile([P, HALF], U32, name="hq%d" % h, align_bytes=64, offset=(8768, 10816)[h])
             hs = ring.tile([P, HALF], U8, name="hs", align_bytes=64)
             nc.vector.quantize_mx(out=hq[:].bitcast(FP8X4), scales=hs[:], in_=h_t[h][:])
             for i in range(4):
-                yT = y_banks[i % 2]
+                yT = banks[(0, 1, 4, 5)[i]]
                 nc.tensor.matmul_mx(out=yT[:], lhsT=hq[:, i * P : (i + 1) * P].bitcast(FP8X4), lhsT_scale=hs[:, i * P : (i + 1) * P],
                                     rhs=wd[:].bitcast(FP8X4), rhs_scale=wds[:], start=True, stop=True)
                 nc.scalar.copy(y_sb[4 * h + i][:], yT[:].rearrange("j (m c) -> j c m", c=4))
 
         def gather_res(c):
-            nc.vector.tensor_copy(r_g[c][:], res[c][:].indirect(offsets[:]))
+            rg = picks.tile([P, J], F32, name="rg%d" % c, align_bytes=64, offset=(8192, 12288, 0, 4096)[c])
+            nc.vector.tensor_copy(rg[:], res[c][:].indirect(offsets[:]))
+            for h in range(2):
+                r_g[(c, h)] = rg[:, h * HALF : (h + 1) * HALF]
 
         def sum_half(c, h):
-            rj = banks[5][:].rearrange("j (i m) -> j i m", i=4)
+            rj = banks[((2, 3, 2, 2), (6, 2, 6, 2))[h][c]][:].rearrange("j (i m) -> j i m", i=4)
             for i in range(4):
-                j0 = (4 * h + i) * P
-                nc.tensor.transpose(rj[:, i, :], r_g[c][:, j0 : j0 + P], ident[:])
-            rs = ring.tile([P, 4, P], F32, name="rs", align_bytes=64)
+                nc.tensor.transpose(rj[:, i, :], r_g[(c, h)][:, i * P : (i + 1) * P], ident[:])
+            rs = keep.tile([P, 4, P], F32, name="rs%d_%d" % (c, h), align_bytes=64)
             nc.scalar.copy(rs[:], rj)
-            zp = banks[6 + c % 2]
+            zp = banks[((6, 7, 3, 3), (7, 3, 7, 3))[h][c]]
             for i in range(4):
-                nc.tensor.matmul(zp[:, i * P : (i + 1) * P], rs[:, i, :], ident[:], start=True, stop=False, is_transpose=True)
-                nc.tensor.matmul(zp[:, i * P : (i + 1) * P], y_sb[4 * h + i][:, c, :], ident[:], start=False, stop=True, is_transpose=True)
+                nc.tensor.matmul(zp[:, i * P : (i + 1) * P], rs[:, i, :], ident[:], start=(i == 0), stop=False, is_transpose=True)
+            for i in range(4):
+                nc.tensor.matmul(zp[:, i * P : (i + 1) * P], y_sb[4 * h + i][:, c, :], ident[:], start=False, stop=(i == 3), is_transpose=True)
             nc.scalar.activation(zs[c][:, h * HALF : (h + 1) * HALF], zp[:], ACT.Identity, bias=bias[:, c : c + 1])
 
         def scatter(c, h):
             cols = slice(h * HALF, (h + 1) * HALF)
-            nc.vector.tensor_tensor(pages[c][:].indirect(offsets[:, 32 * h : 32 * h + 32]), zs[c][:, cols], gate[:, cols], MULT)
+            nc.vector.tensor_tensor(pages[c][:].indirect(half_offsets[h]), zs[c][:, cols], gate[:, cols], MULT)
 
-        up_pair(0, banks[0:2], banks[2])
-        up_pair(1, banks[0:2], banks[3])
-
+        up_pair(0)
+        up_pair(1)
         gather_res(0)
-        load_res(3)
-        gather_res(1)
-        gate = reuse.tile([P, J], F32, name="gate", align_bytes=64, offset=10752)
+        gate = reuse.tile([P, J], F32, name="gate", align_bytes=64, offset=0)
         nc.sync.dma_start(gate[:], wgo)
-        down_half(0, banks[0:2])
+        gather_res(1)
+        down_half(0)
         gather_res(2)
         gather_res(3)
-        sum_half(0, 0)
-
-        scatter(0, 0)
-        up_pair(2, banks[2:4], banks[4])
-        sum_half(1, 0)
-        scatter(1, 0)
-        up_pair(3, banks[0:2], banks[2])
-        down_half(1, banks[3:5])
+        for i in range(2):
+            page = reuse.tile([P, T], F32, name="page%d" % (2 + i), align_bytes=64, offset=(27200, 35392)[i])
+            nc.gpsimd.memset(page[:], 0.0)
+            pages.append(page)
+        for c in range(2):
+            sum_half(c, 0)
+            scatter(c, 0)
+        up_pair(2)
+        up_pair(3)
         for c in range(2, 4):
             sum_half(c, 0)
             scatter(c, 0)
+        down_half(1)
         for c in range(4):
             sum_half(c, 1)
             scatter(c, 1)

@@ -48,7 +48,7 @@ def tile_list_modp_relu_resb_kernel(tc, tab_words, tab_scales, wu_words, wu_scal
         ident = keep.tile([P, P], F32, name="ident", align_bytes=64)
         make_identity(nc, ident[:])
         pages = []
-        for i in range(2):
+        for i in range(3):
             page = keep.tile([P, T], F32, name="page%d" % i, align_bytes=64)
             nc.vector.memset(page[:], 0.0)
             pages.append(page)
@@ -157,10 +157,9 @@ def tile_list_modp_relu_resb_kernel(tc, tab_words, tab_scales, wu_words, wu_scal
         down_half(0)
         gather_res(2)
         gather_res(3)
-        for i in range(2):
-            page = reuse.tile([P, T], F32, name="page%d" % (2 + i), align_bytes=64, offset=(27200, 35392)[i])
-            nc.gpsimd.memset(page[:], 0.0)
-            pages.append(page)
+        page = reuse.tile([P, T], F32, name="page3", align_bytes=64, offset=31296)
+        nc.vector.memset(page[:], 0.0)
+        pages.append(page)
         for c in range(2):
             sum_half(c, 0)
             scatter(c, 0)

@@ -16,6 +16,7 @@ FP8X4 = mybir.dt.float8_e4m3fn_x4
 FP4X4 = mybir.dt.float4_e2m1fn_x4
 ACT = mybir.ActivationFunctionType
 MULT = mybir.AluOpType.mult
+ADD = mybir.AluOpType.add
 
 P = 128
 HALF = J // 2
@@ -35,141 +36,167 @@ def tile_list_modp_relu_resb_kernel(tc, tab_words, tab_scales, wu_words, wu_scal
         nc.sync.dma_start(offsets[:], offs)
         half_offsets = [offsets[:, 32 * h : 32 * h + 32] for h in range(2)]
 
-        r_rows = rT.rearrange("(p c) t -> p c t", c=4)
-        out_rows = out.rearrange("(p c) t -> p c t", c=4)
-
-        tabs = reuse.tile([P, T], U8, name="tabs", align_bytes=64, offset=7680)
+        tabs = keep.tile([P, T], U8, name="tabs", align_bytes=64)
         nc.vector.memset(tabs[:].bitcast(I32), 0)
         wus = keep.tile([P, 2, R], U8, name="wus", align_bytes=64)
         nc.vector.memset(wus[:].bitcast(I32), 0)
-        plane1 = [keep.tile([P, HALF], U8, name="plane1_%d" % h, align_bytes=64) for h in range(2)]
-        for h in range(2):
-            nc.vector.memset(plane1[h][:].bitcast(I32), 0)
+        plane1 = keep.tile([P, J], U8, name="plane1", align_bytes=64)
+        nc.vector.memset(plane1[:].bitcast(I32), 0)
+        brow = keep.tile([P, P], F32, name="brow", align_bytes=64)
+        nc.gpsimd.memset(brow[:], 0.0)
+        nc.scalar.dma_start(brow[0:4, :], b.rearrange("(c m) -> c m", c=4))
+        wds = keep.tile([P, N], U8, name="wds", align_bytes=64)
+        nc.gpsimd.memset(wds[:].bitcast(I32), 0)
+        for q in range(4):
+            nc.gpsimd.dma_start(wds[32 * q : 32 * q + 4, :].bitcast(I32), wd_scales[0, 4 * q : 4 * q + 4, :].bitcast(I32))
         ident = keep.tile([P, P], F32, name="ident", align_bytes=64)
         make_identity(nc, ident[:])
         pages = []
-        for i in range(3):
+        for i in range(2):
             page = keep.tile([P, T], F32, name="page%d" % i, align_bytes=64)
             nc.vector.memset(page[:], 0.0)
             pages.append(page)
 
         wu = keep.tile([P, 2, 2 * R], U8, name="wu", align_bytes=64)
-        tabw = [reuse.tile([P, T], I32, name="tabw%d" % a, align_bytes=64, offset=(16960, 31296)[a]) for a in range(2)]
-        res = []
+        tabw = [keep.tile([P, T], I32, name="tabw%d" % a, align_bytes=64) for a in range(2)]
+        res = {}
 
         def load_res(c):
-            rt = reuse.tile([P, T], F32, name="res%d" % c, align_bytes=64, offset=(0, 8768, 19008, 31296)[c])
-            nc.sync.dma_start(rt[:], r_rows[:, c, :])
-            res.append(rt)
+            res[c] = keep.tile([P, T], F32, name="res%d" % c, align_bytes=64)
+            nc.sync.dma_start(res[c][:], rT[c * P : (c + 1) * P, :])
 
         nc.sync.dma_start(wu[:].bitcast(I32), wu_words.rearrange("a p n -> p a n").bitcast(I32))
-        for q in range(4):
-            nc.sync.dma_start(tabs[32 * q : 32 * q + 8, :].bitcast(I32), tab_scales[:, 4 * q : 4 * q + 4, :].bitcast(I32))
-        for a in range(2):
-            nc.sync.dma_start(tabw[a][:], tab_words[a].rearrange("p t i -> p (t i)").bitcast(I32))
+        scale_rows = tab_scales.rearrange("a (q r) t -> r q a t", r=4)
+        for r in range(4):
+            nc.sync.dma_start(tabs[r:P:16, :].bitcast(I32), scale_rows[r].bitcast(I32))
+        nc.sync.dma_start(tabw[0][:], tab_words[0].rearrange("p t i -> p (t i)").bitcast(I32))
         for q in range(4):
             nc.sync.dma_start(wus[32 * q : 32 * q + 4, :, :].bitcast(I32), wu_scales[:, 4 * q : 4 * q + 4, :].rearrange("a r n -> r a n").bitcast(I32))
+        nc.sync.dma_start(tabw[1][:], tab_words[1].rearrange("p t i -> p (t i)").bitcast(I32))
 
-        plane0 = [keep.tile([P, HALF], U8, name="plane0_%d" % h, align_bytes=64) for h in range(2)]
-        for h in range(2):
-            nc.vector.tensor_copy(plane0[h][:], tabs[:].indirect(half_offsets[h]))
-            nc.scalar.dma_start(plane1[h][0:112, :].bitcast(I32), plane0[h][4:116, :].bitcast(I32))
+        plane0 = keep.tile([P, J], U8, name="plane0", align_bytes=64)
+        nc.vector.tensor_copy(plane0[:], tabs[:].indirect(offsets[:]))
+        nc.sync.dma_start(plane1[0:100, :].bitcast(I32), plane0[16:116, :].bitcast(I32))
         planes = [plane0, plane1]
+        load_res(2)
+        wd = keep.tile([P, N], I32, name="wd", align_bytes=64)
+        nc.sync.dma_start(wd[:], wd_words[0].rearrange("p n i -> p (n i)").bitcast(I32))
+        load_res(3)
         load_res(0)
+        gate = keep.tile([P, J], F32, name="gate", align_bytes=64)
+        nc.sync.dma_start(gate[:], wgo)
         load_res(1)
-        wds = reuse.tile([P, N], U8, name="wds", align_bytes=64, offset=8192)
-        nc.vector.memset(wds[:].bitcast(I32), 0)
-        for q in range(4):
-            nc.sync.dma_start(wds[32 * q : 32 * q + 4, :].bitcast(I32), wd_scales[0, 4 * q : 4 * q + 4, :].bitcast(I32))
+
 
         words = [[keep.tile([P, HALF], U32, name="words%d_%d" % (a, h), align_bytes=64) for h in range(2)] for a in range(2)]
-        for h in range(2):
-            for a in range(2):
+        for a in range(2):
+            for h in range(2):
                 nc.vector.tensor_copy(words[a][h][:], tabw[a][:].bitcast(U32).indirect(half_offsets[h]))
-        bias = reuse.tile([P, 4], F32, name="bias", align_bytes=64, offset=8704)
-        nc.sync.dma_start(bias[:], b.rearrange("(p c) -> p c", c=4))
-        wd = reuse.tile([P, N], I32, name="wd", align_bytes=64, offset=16960)
-        nc.sync.dma_start(wd[:], wd_words[0].rearrange("p n i -> p (n i)").bitcast(I32))
-        load_res(2)
-        load_res(3)
 
-        y_sb = [keep.tile([P, 4, P], F32, name="ys%d" % i, align_bytes=64) for i in range(8)]
-        zs = [keep.tile([P, J], F32, name="z%d" % c, align_bytes=64) for c in range(4)]
-        r_g = {}
-        h_t = [picks.tile([P, HALF * 4], BF16, name="hT%d" % h, align_bytes=64, offset=(2048, 16384)[h]) for h in range(2)]
+        bias = keep.tile([P, 4], F32, name="bias", align_bytes=64)
 
-        def up_pair(g):
-            xt = banks[2 + g % 2][:].rearrange("p (i u j) -> p i u j", i=2, u=2)
-            h = g // 2
-            for i in range(2):
-                j0 = (2 * (g % 2) + i) * P
-                cols = slice(j0, j0 + P)
-                aT = banks[5 * h + i]
-                for a in range(2):
-                    nc.tensor.matmul_mx(out=aT[:], lhsT=words[a][h][:, cols].bitcast(FP8X4), lhsT_scale=planes[a][h][:, cols],
-                                        rhs=wu[:, a, :].bitcast(FP4X4), rhs_scale=wus[:, a, :], start=(a == 0), stop=(a == 1))
-                hb = ring.tile([P, 2, P, 2], BF16, name="hb", align_bytes=64)
-                nc.scalar.activation(hb[:], aT[:].rearrange("j (p u e) -> j u p e", u=2, e=2), ACT.Relu)
-                hw = hb[:].rearrange("j u p e -> j (u p e)").bitcast(F32)
-                for u in range(2):
-                    nc.tensor.transpose(xt[:, i, u, :], hw[:, u * P : (u + 1) * P], ident[:])
-            nc.scalar.copy(h_t[h][:].bitcast(F32)[:, (g % 2) * 4 * P : (g % 2 + 1) * 4 * P].rearrange("p (i j u) -> p i j u", i=2, u=2), xt.rearrange("p i u j -> p i j u"))
+        y_sb = [keep.tile([P, J], F32, name="y%d" % c, align_bytes=64) for c in range(4)]
+        zs = {c: keep.tile([P, J], F32, name="z%d" % c, align_bytes=64)[:] for c in range(1, 4)}
+        z0 = [reuse.tile([P, HALF], F32, name="z0_%d" % h, align_bytes=64, offset=2048 * h) for h in range(2)]
+        h_t = [picks.tile([P, HALF * 4], BF16, name="hT%d" % h, align_bytes=64, offset=4096 * h) for h in range(2)]
+        picked = {}
 
-        def down_half(h):
-            hq = reuse.tile([P, HALF], U32, name="hq%d" % h, align_bytes=64, offset=(8768, 10816)[h])
+        def up_half(h):
+            up_banks = (banks[0:4], [banks[4], banks[5], banks[6], banks[7]])[h]
+            order = ([(a, i) for a in range(2) for i in range(4)], [(a, i) for i in range(4) for a in range(2)])[h]
+            hbs = []
+            for a, i in order:
+                cols = slice(i * P, (i + 1) * P)
+                pcols = slice(h * HALF + i * P, h * HALF + (i + 1) * P)
+                nc.tensor.matmul_mx(out=up_banks[i][:], lhsT=words[a][h][:, cols].bitcast(FP8X4), lhsT_scale=planes[a][:, pcols],
+                                    rhs=wu[:, a, :].bitcast(FP4X4), rhs_scale=wus[:, a, :], start=(a == 0), stop=(a == 1))
+                if a == 1:
+                    hb = ring.tile([P, 2, P, 2], BF16, name="hb", align_bytes=64, bufs=4)
+                    nc.scalar.activation(hb[:], up_banks[i][:].rearrange("j (p u e) -> j u p e", u=2, e=2), ACT.Relu)
+                    hbs.append(hb)
+            for g in range(2):
+                xt = banks[(4, 0)[h] + g][:].rearrange("p (i u j) -> p i u j", i=2, u=2)
+                for i in range(2):
+                    hw = hbs[2 * g + i][:].rearrange("j u p e -> j (u p e)").bitcast(F32)
+                    for u in range(2):
+                        nc.tensor.transpose(xt[:, i, u, :], hw[:, u * P : (u + 1) * P], ident[:])
+                nc.scalar.copy(h_t[h][:].bitcast(F32)[:, g * 4 * P : (g + 1) * 4 * P].rearrange("p (i j u) -> p i j u", i=2, u=2), xt.rearrange("p i u j -> p i j u"))
+
+        coded = {}
+
+        def quantise(h):
+            hq = reuse.tile([P, HALF], U32, name="hq%d" % h, align_bytes=64, offset=(4096, 0)[h])
             hs = ring.tile([P, HALF], U8, name="hs", align_bytes=64)
             nc.vector.quantize_mx(out=hq[:].bitcast(FP8X4), scales=hs[:], in_=h_t[h][:])
-            for i in range(4):
-                yT = banks[(0, 1, 4, 5)[i]]
-                nc.tensor.matmul_mx(out=yT[:], lhsT=hq[:, i * P : (i + 1) * P].bitcast(FP8X4), lhsT_scale=hs[:, i * P : (i + 1) * P],
-                                    rhs=wd[:].bitcast(FP8X4), rhs_scale=wds[:], start=True, stop=True)
-                nc.scalar.copy(y_sb[4 * h + i][:], yT[:].rearrange("j (m c) -> j c m", c=4))
+            coded[h] = (hq, hs)
 
-        def gather_res(c):
-            rg = picks.tile([P, J], F32, name="rg%d" % c, align_bytes=64, offset=(8192, 12288, 0, 4096)[c])
-            nc.vector.tensor_copy(rg[:], res[c][:].indirect(offsets[:]))
-            for h in range(2):
-                r_g[(c, h)] = rg[:, h * HALF : (h + 1) * HALF]
+        def down(c, h, bank):
+            hq, hs = coded[h]
+            nc.tensor.matmul_mx(out=banks[bank][:], lhsT=wd[:, c * P : (c + 1) * P].bitcast(FP8X4), lhsT_scale=wds[:, c * P : (c + 1) * P],
+                                rhs=hq[:].bitcast(FP8X4), rhs_scale=hs[:], start=True, stop=True)
+            nc.scalar.activation(y_sb[c][:, h * HALF : (h + 1) * HALF], banks[bank][:], ACT.Identity, bias=bias[:, c : c + 1])
+
+        def span(h):
+            return (offsets[:], slice(0, J)) if h is None else (half_offsets[h], slice(h * HALF, (h + 1) * HALF))
+
+        def gather_add(c, h):
+            lst, cols = span(h)
+            nc.vector.tensor_tensor(z0[h][:] if c == 0 else zs[c][:, cols], res[c][:].indirect(lst), y_sb[c][:, cols], ADD)
+
+        def gather_plain(c, j0, j1, offset):
+            rg = picks.tile([P, j1 - j0], F32, name="rg%d_%d" % (c, j0), align_bytes=64, offset=offset)
+            nc.vector.tensor_copy(rg[:], res[c][:].indirect(offsets[:, j0 // 16 : j1 // 16]))
+            for j in range(j0, j1, P):
+                picked[(c, j // P)] = rg[:, j - j0 : j - j0 + P]
 
         def sum_half(c, h):
-            rj = banks[((2, 3, 2, 2), (6, 2, 6, 2))[h][c]][:].rearrange("j (i m) -> j i m", i=4)
+            across = banks[(3, 2 * (c % 2))[h]]
             for i in range(4):
-                nc.tensor.transpose(rj[:, i, :], r_g[(c, h)][:, i * P : (i + 1) * P], ident[:])
-            rs = keep.tile([P, 4, P], F32, name="rs%d_%d" % (c, h), align_bytes=64)
-            nc.scalar.copy(rs[:], rj)
-            zp = banks[((6, 7, 3, 3), (7, 3, 7, 3))[h][c]]
+                nc.tensor.matmul(across[:, i * P : (i + 1) * P], picked[(c, 4 * h + i)], ident[:], start=(i == 0), stop=False, is_transpose=True)
             for i in range(4):
-                nc.tensor.matmul(zp[:, i * P : (i + 1) * P], rs[:, i, :], ident[:], start=(i == 0), stop=False, is_transpose=True)
+                nc.tensor.matmul(across[:, i * P : (i + 1) * P], y_sb[c][:, h * HALF + i * P : h * HALF + (i + 1) * P], ident[:], start=False, stop=(i == 3), is_transpose=True)
+            turned = ring.tile([P, HALF], F32, name="turned", align_bytes=64)
+            nc.scalar.copy(turned[:], across[:])
+            back = banks[(2, 2 * (c % 2) + 1)[h]]
             for i in range(4):
-                nc.tensor.matmul(zp[:, i * P : (i + 1) * P], y_sb[4 * h + i][:, c, :], ident[:], start=False, stop=(i == 3), is_transpose=True)
-            nc.scalar.activation(zs[c][:, h * HALF : (h + 1) * HALF], zp[:], ACT.Identity, bias=bias[:, c : c + 1])
+                nc.tensor.transpose(back[:, i * P : (i + 1) * P], turned[:, i * P : (i + 1) * P], ident[:])
+            nc.scalar.copy(zs[c][:, h * HALF : (h + 1) * HALF], back[:])
 
         def scatter(c, h):
-            cols = slice(h * HALF, (h + 1) * HALF)
-            nc.vector.tensor_tensor(pages[c][:].indirect(half_offsets[h]), zs[c][:, cols], gate[:, cols], MULT)
+            lst, cols = span(h)
+            nc.vector.tensor_tensor(pages[c // 2][:].indirect(lst), z0[h][:] if c == 0 else zs[c][:, cols], gate[:, cols], MULT)
 
-        up_pair(0)
-        up_pair(1)
-        gather_res(0)
-        gate = reuse.tile([P, J], F32, name="gate", align_bytes=64, offset=0)
-        nc.sync.dma_start(gate[:], wgo)
-        gather_res(1)
-        down_half(0)
-        gather_res(2)
-        gather_res(3)
-        page = reuse.tile([P, T], F32, name="page3", align_bytes=64, offset=31296)
-        nc.vector.memset(page[:], 0.0)
-        pages.append(page)
-        for c in range(2):
-            sum_half(c, 0)
-            scatter(c, 0)
-        up_pair(2)
-        up_pair(3)
-        for c in range(2, 4):
-            sum_half(c, 0)
-            scatter(c, 0)
-        down_half(1)
-        for c in range(4):
-            sum_half(c, 1)
-            scatter(c, 1)
-            nc.sync.dma_start(out_rows[:, c, :], pages[c][:])
+        def store(c):
+            nc.sync.dma_start(out[c * P : (c + 1) * P, :], pages[c // 2][:])
+
+        up_half(0)
+        nc.tensor.transpose(banks[2][:, 0:P], brow[:], ident[:])
+        nc.scalar.copy(bias[:], banks[2][:, 0:4])
+        gather_plain(2, 0, J, 8192)
+        quantise(0)
+        down(0, 0, 6)
+        down(2, 0, 7)
+        gather_plain(3, 0, J, 12288)
+        up_half(1)
+        gather_add(0, 0)
+        sum_half(2, 0)
+        scatter(0, 0)
+        down(1, 0, 6)
+        down(3, 0, 7)
+        sum_half(3, 0)
+        quantise(1)
+        for c in (0, 2, 1, 3):
+            down(c, 1, 4 + c)
+        scatter(2, 0)
+        gather_add(0, 1)
+        gather_add(1, 0)
+        sum_half(2, 1)
+        scatter(0, 1)
+        store(0)
+        gather_add(1, 1)
+        sum_half(3, 1)
+        scatter(2, 1)
+        store(2)
+        for c in (1, 3):
+            scatter(c, None)
+            store(c)

@@ -37,14 +37,14 @@ def tile_list_modp_relu_resb_kernel(tc, tab_words, tab_scales, wu_words, wu_scal
         half_offsets = [offsets[:, 32 * h : 32 * h + 32] for h in range(2)]
 
         tabs = keep.tile([P, T], U8, name="tabs", align_bytes=64)
-        nc.vector.memset(tabs[:].bitcast(I32), 0)
+        nc.gpsimd.memset(tabs[:, 0 : T // 2].bitcast(I32), 0)
+        nc.vector.memset(tabs[:, T // 2 : T].bitcast(I32), 0)
         wus = keep.tile([P, 2, R], U8, name="wus", align_bytes=64)
+        brow = keep.tile([P, P], F32, name="brow", align_bytes=64)
+        nc.vector.memset(brow[:], 0.0)
         nc.vector.memset(wus[:].bitcast(I32), 0)
         plane1 = keep.tile([P, J], U8, name="plane1", align_bytes=64)
         nc.vector.memset(plane1[:].bitcast(I32), 0)
-        brow = keep.tile([P, P], F32, name="brow", align_bytes=64)
-        nc.gpsimd.memset(brow[:], 0.0)
-        nc.scalar.dma_start(brow[0:4, :], b.rearrange("(c m) -> c m", c=4))
         wds = keep.tile([P, N], U8, name="wds", align_bytes=64)
         nc.gpsimd.memset(wds[:].bitcast(I32), 0)
         for q in range(4):
@@ -68,19 +68,21 @@ def tile_list_modp_relu_resb_kernel(tc, tab_words, tab_scales, wu_words, wu_scal
         nc.sync.dma_start(wu[:].bitcast(I32), wu_words.rearrange("a p n -> p a n").bitcast(I32))
         scale_rows = tab_scales.rearrange("a (q r) t -> r q a t", r=4)
         for r in range(4):
-            nc.sync.dma_start(tabs[r:P:16, :].bitcast(I32), scale_rows[r].bitcast(I32))
+            (nc.sync, nc.scalar)[r % 2].dma_start(tabs[r:P:16, :].bitcast(I32), scale_rows[r].bitcast(I32))
+        nc.scalar.dma_start(brow[0:4, :], b.rearrange("(c m) -> c m", c=4))
         nc.sync.dma_start(tabw[0][:], tab_words[0].rearrange("p t i -> p (t i)").bitcast(I32))
         for q in range(4):
             nc.sync.dma_start(wus[32 * q : 32 * q + 4, :, :].bitcast(I32), wu_scales[:, 4 * q : 4 * q + 4, :].rearrange("a r n -> r a n").bitcast(I32))
         nc.sync.dma_start(tabw[1][:], tab_words[1].rearrange("p t i -> p (t i)").bitcast(I32))
+
+        wd = keep.tile([P, N], I32, name="wd", align_bytes=64)
+        nc.sync.dma_start(wd[:], wd_words[0].rearrange("p n i -> p (n i)").bitcast(I32))
 
         plane0 = keep.tile([P, J], U8, name="plane0", align_bytes=64)
         nc.vector.tensor_copy(plane0[:], tabs[:].indirect(offsets[:]))
         nc.sync.dma_start(plane1[0:100, :].bitcast(I32), plane0[16:116, :].bitcast(I32))
         planes = [plane0, plane1]
         load_res(2)
-        wd = keep.tile([P, N], I32, name="wd", align_bytes=64)
-        nc.sync.dma_start(wd[:], wd_words[0].rearrange("p n i -> p (n i)").bitcast(I32))
         load_res(3)
         load_res(0)
         gate = keep.tile([P, J], F32, name="gate", align_bytes=64)
@@ -102,7 +104,7 @@ def tile_list_modp_relu_resb_kernel(tc, tab_words, tab_scales, wu_words, wu_scal
         picked = {}
 
         def up_half(h):
-            up_banks = (banks[0:4], [banks[4], banks[5], banks[6], banks[7]])[h]
+            up_banks = (banks[0:4], [banks[4], banks[6], banks[7], banks[6]])[h]
             order = ([(a, i) for a in range(2) for i in range(4)], [(a, i) for i in range(4) for a in range(2)])[h]
             hbs = []
             for a, i in order:
@@ -173,15 +175,16 @@ def tile_list_modp_relu_resb_kernel(tc, tab_words, tab_scales, wu_words, wu_scal
         nc.tensor.transpose(banks[2][:, 0:P], brow[:], ident[:])
         nc.scalar.copy(bias[:], banks[2][:, 0:4])
         gather_plain(2, 0, J, 8192)
+        gather_plain(3, 0, 256, 12288)
         quantise(0)
         down(0, 0, 6)
         down(2, 0, 7)
-        gather_plain(3, 0, J, 12288)
+        gather_plain(3, 256, J, 0)
         up_half(1)
         gather_add(0, 0)
         sum_half(2, 0)
         scatter(0, 0)
-        down(1, 0, 6)
+        down(1, 0, 5)
         down(3, 0, 7)
         sum_half(3, 0)
         quantise(1)

@@ -47,8 +47,6 @@ def tile_list_modp_relu_resb_kernel(tc, tab_words, tab_scales, wu_words, wu_scal
         nc.vector.memset(plane1[:].bitcast(I32), 0)
         wds = keep.tile([P, N], U8, name="wds", align_bytes=64)
         nc.gpsimd.memset(wds[:].bitcast(I32), 0)
-        for q in range(4):
-            nc.gpsimd.dma_start(wds[32 * q : 32 * q + 4, :].bitcast(I32), wd_scales[0, 4 * q : 4 * q + 4, :].bitcast(I32))
         ident = keep.tile([P, P], F32, name="ident", align_bytes=64)
         make_identity(nc, ident[:])
         pages = []
@@ -75,8 +73,8 @@ def tile_list_modp_relu_resb_kernel(tc, tab_words, tab_scales, wu_words, wu_scal
             nc.sync.dma_start(wus[32 * q : 32 * q + 4, :, :].bitcast(I32), wu_scales[:, 4 * q : 4 * q + 4, :].rearrange("a r n -> r a n").bitcast(I32))
         nc.sync.dma_start(tabw[1][:], tab_words[1].rearrange("p t i -> p (t i)").bitcast(I32))
 
-        wd = keep.tile([P, N], I32, name="wd", align_bytes=64)
-        nc.sync.dma_start(wd[:], wd_words[0].rearrange("p n i -> p (n i)").bitcast(I32))
+        for q in range(4):
+            nc.sync.dma_start(wds[32 * q : 32 * q + 4, :].bitcast(I32), wd_scales[0, 4 * q : 4 * q + 4, :].bitcast(I32))
 
         plane0 = keep.tile([P, J], U8, name="plane0", align_bytes=64)
         nc.vector.tensor_copy(plane0[:], tabs[:].indirect(offsets[:]))
@@ -84,10 +82,13 @@ def tile_list_modp_relu_resb_kernel(tc, tab_words, tab_scales, wu_words, wu_scal
         planes = [plane0, plane1]
         load_res(2)
         load_res(3)
+        wd = keep.tile([P, N], I32, name="wd", align_bytes=64)
+        nc.sync.dma_start(wd[:], wd_words[0].rearrange("p n i -> p (n i)").bitcast(I32))
         load_res(0)
         gate = keep.tile([P, J], F32, name="gate", align_bytes=64)
-        nc.sync.dma_start(gate[:], wgo)
+        nc.sync.dma_start(gate[:, 0:HALF], wgo[:, 0:HALF])
         load_res(1)
+        nc.sync.dma_start(gate[:, HALF:J], wgo[:, HALF:J])
 
 
         words = [[keep.tile([P, HALF], U32, name="words%d_%d" % (a, h), align_bytes=64) for h in range(2)] for a in range(2)]

@@ -36,7 +36,7 @@ def tile_list_modp_relu_resb_kernel(tc, tab_words, tab_scales, wu_words, wu_scal
         nc.sync.dma_start(offsets[:], offs)
         half_offsets = [offsets[:, 32 * h : 32 * h + 32] for h in range(2)]
 
-        tabs = keep.tile([P, T], U8, name="tabs", align_bytes=64)
+        tabs = reuse.tile([P, T], U8, name="tabs", align_bytes=64, offset=15360)
         nc.gpsimd.memset(tabs[:, 0 : T // 2].bitcast(I32), 0)
         nc.vector.memset(tabs[:, T // 2 : T].bitcast(I32), 0)
         wus = keep.tile([P, 2, R], U8, name="wus", align_bytes=64)
@@ -49,11 +49,6 @@ def tile_list_modp_relu_resb_kernel(tc, tab_words, tab_scales, wu_words, wu_scal
         nc.gpsimd.memset(wds[:].bitcast(I32), 0)
         ident = keep.tile([P, P], F32, name="ident", align_bytes=64)
         make_identity(nc, ident[:])
-        pages = []
-        for i in range(2):
-            page = keep.tile([P, T], F32, name="page%d" % i, align_bytes=64)
-            nc.vector.memset(page[:], 0.0)
-            pages.append(page)
 
         wu = keep.tile([P, 2, 2 * R], U8, name="wu", align_bytes=64)
         tabw = [keep.tile([P, T], I32, name="tabw%d" % a, align_bytes=64) for a in range(2)]
@@ -80,6 +75,11 @@ def tile_list_modp_relu_resb_kernel(tc, tab_words, tab_scales, wu_words, wu_scal
         nc.vector.tensor_copy(plane0[:], tabs[:].indirect(offsets[:]))
         nc.sync.dma_start(plane1[0:100, :].bitcast(I32), plane0[16:116, :].bitcast(I32))
         planes = [plane0, plane1]
+        pages = []
+        for i in range(2):
+            page = reuse.tile([P, T], F32, name="page%d" % i, align_bytes=64, offset=8192 * (i + 1))
+            nc.gpsimd.memset(page[:], 0.0)
+            pages.append(page)
         load_res(2)
         load_res(3)
         wd = keep.tile([P, N], I32, name="wd", align_bytes=64)

@@ -47,6 +47,8 @@ def tile_list_modp_relu_resb_kernel(tc, tab_words, tab_scales, wu_words, wu_scal
         nc.vector.memset(plane1[:].bitcast(I32), 0)
         wds = keep.tile([P, N], U8, name="wds", align_bytes=64)
         nc.gpsimd.memset(wds[:].bitcast(I32), 0)
+        for q in range(4):
+            nc.gpsimd.dma_start(wds[32 * q : 32 * q + 4, :].bitcast(I32), wd_scales[0, 4 * q : 4 * q + 4, :].bitcast(I32))
         ident = keep.tile([P, P], F32, name="ident", align_bytes=64)
         make_identity(nc, ident[:])
 
@@ -61,19 +63,18 @@ def tile_list_modp_relu_resb_kernel(tc, tab_words, tab_scales, wu_words, wu_scal
         nc.sync.dma_start(wu[:].bitcast(I32), wu_words.rearrange("a p n -> p a n").bitcast(I32))
         scale_rows = tab_scales.rearrange("a (q r) t -> r q a t", r=4)
         for r in range(4):
-            (nc.sync, nc.scalar)[r % 2].dma_start(tabs[r:P:16, :].bitcast(I32), scale_rows[r].bitcast(I32))
+            nc.sync.dma_start(tabs[r:P:16, :].bitcast(I32), scale_rows[r].bitcast(I32))
         nc.scalar.dma_start(brow[0:4, :], b.rearrange("(c m) -> c m", c=4))
         nc.sync.dma_start(tabw[0][:], tab_words[0].rearrange("p t i -> p (t i)").bitcast(I32))
         for q in range(4):
             nc.sync.dma_start(wus[32 * q : 32 * q + 4, :, :].bitcast(I32), wu_scales[:, 4 * q : 4 * q + 4, :].rearrange("a r n -> r a n").bitcast(I32))
         nc.sync.dma_start(tabw[1][:], tab_words[1].rearrange("p t i -> p (t i)").bitcast(I32))
 
-        for q in range(4):
-            nc.sync.dma_start(wds[32 * q : 32 * q + 4, :].bitcast(I32), wd_scales[0, 4 * q : 4 * q + 4, :].bitcast(I32))
 
         plane0 = keep.tile([P, J], U8, name="plane0", align_bytes=64)
         nc.vector.tensor_copy(plane0[:], tabs[:].indirect(offsets[:]))
-        nc.sync.dma_start(plane1[0:100, :].bitcast(I32), plane0[16:116, :].bitcast(I32))
+        for q in range(4):
+            nc.sync.dma_start(plane1[32 * q : 32 * q + 4, :].bitcast(I32), plane0[32 * q + 16 : 32 * q + 20, :].bitcast(I32))
         planes = [plane0, plane1]
         pages = []
         for i in range(2):

@@ -20,6 +20,7 @@ ADD = mybir.AluOpType.add
 
 P = 128
 HALF = J // 2
+QUARTER = J // 4
 
 
 def tile_list_modp_relu_resb_kernel(tc, tab_words, tab_scales, wu_words, wu_scales, wd_words, wd_scales, rT, b, wgo, offs, out):
@@ -52,7 +53,7 @@ def tile_list_modp_relu_resb_kernel(tc, tab_words, tab_scales, wu_words, wu_scal
         ident = keep.tile([P, P], F32, name="ident", align_bytes=64)
         make_identity(nc, ident[:])
 
-        wu = keep.tile([P, 2, 2 * R], U8, name="wu", align_bytes=64)
+        wu = [keep.tile([P, 2 * R], U8, name="wu%d" % a, align_bytes=64) for a in range(2)]
         tabw = [keep.tile([P, T], I32, name="tabw%d" % a, align_bytes=64) for a in range(2)]
         res = {}
 
@@ -60,7 +61,7 @@ def tile_list_modp_relu_resb_kernel(tc, tab_words, tab_scales, wu_words, wu_scal
             res[c] = keep.tile([P, T], F32, name="res%d" % c, align_bytes=64)
             nc.sync.dma_start(res[c][:], rT[c * P : (c + 1) * P, :])
 
-        nc.sync.dma_start(wu[:].bitcast(I32), wu_words.rearrange("a p n -> p a n").bitcast(I32))
+        nc.sync.dma_start(wu[0][:].bitcast(I32), wu_words[0].bitcast(I32))
         scale_rows = tab_scales.rearrange("a (q r) t -> r q a t", r=4)
         for r in range(4):
             nc.sync.dma_start(tabs[r:P:16, :].bitcast(I32), scale_rows[r].bitcast(I32))
@@ -69,6 +70,7 @@ def tile_list_modp_relu_resb_kernel(tc, tab_words, tab_scales, wu_words, wu_scal
         for q in range(4):
             nc.sync.dma_start(wus[32 * q : 32 * q + 4, :, :].bitcast(I32), wu_scales[:, 4 * q : 4 * q + 4, :].rearrange("a r n -> r a n").bitcast(I32))
         nc.sync.dma_start(tabw[1][:], tab_words[1].rearrange("p t i -> p (t i)").bitcast(I32))
+        nc.sync.dma_start(wu[1][:].bitcast(I32), wu_words[1].bitcast(I32))
 
 
         plane0 = keep.tile([P, J], U8, name="plane0", align_bytes=64)
@@ -92,10 +94,13 @@ def tile_list_modp_relu_resb_kernel(tc, tab_words, tab_scales, wu_words, wu_scal
         nc.sync.dma_start(gate[:, HALF:J], wgo[:, HALF:J])
 
 
-        words = [[keep.tile([P, HALF], U32, name="words%d_%d" % (a, h), align_bytes=64) for h in range(2)] for a in range(2)]
+        words = {}
         for a in range(2):
-            for h in range(2):
-                nc.vector.tensor_copy(words[a][h][:], tabw[a][:].bitcast(U32).indirect(half_offsets[h]))
+            for j0, j1 in ((0, QUARTER), (QUARTER, HALF), (HALF, J)):
+                wt = keep.tile([P, j1 - j0], U32, name="words%d_%d" % (a, j0), align_bytes=64)
+                nc.vector.tensor_copy(wt[:], tabw[a][:].bitcast(U32).indirect(offsets[:, j0 // 16 : j1 // 16]))
+                for j in range(j0, j1, P):
+                    words[(a, j // P)] = wt[:, j - j0 : j - j0 + P]
 
         bias = keep.tile([P, 4], F32, name="bias", align_bytes=64)
 
@@ -110,10 +115,9 @@ def tile_list_modp_relu_resb_kernel(tc, tab_words, tab_scales, wu_words, wu_scal
             order = ([(a, i) for a in range(2) for i in range(4)], [(a, i) for i in range(4) for a in range(2)])[h]
             hbs = []
             for a, i in order:
-                cols = slice(i * P, (i + 1) * P)
                 pcols = slice(h * HALF + i * P, h * HALF + (i + 1) * P)
-                nc.tensor.matmul_mx(out=up_banks[i][:], lhsT=words[a][h][:, cols].bitcast(FP8X4), lhsT_scale=planes[a][:, pcols],
-                                    rhs=wu[:, a, :].bitcast(FP4X4), rhs_scale=wus[:, a, :], start=(a == 0), stop=(a == 1))
+                nc.tensor.matmul_mx(out=up_banks[i][:], lhsT=words[(a, 4 * h + i)].bitcast(FP8X4), lhsT_scale=planes[a][:, pcols],
+                                    rhs=wu[a][:].bitcast(FP4X4), rhs_scale=wus[:, a, :], start=(a == 0), stop=(a == 1))
                 if a == 1:
                     hb = ring.tile([P, 2, P, 2], BF16, name="hb", align_bytes=64, bufs=4)
                     nc.scalar.activation(hb[:], up_banks[i][:].rearrange("j (p u e) -> j u p e", u=2, e=2), ACT.Relu)
@@ -177,11 +181,11 @@ def tile_list_modp_relu_resb_kernel(tc, tab_words, tab_scales, wu_words, wu_scal
         nc.tensor.transpose(banks[2][:, 0:P], brow[:], ident[:])
         nc.scalar.copy(bias[:], banks[2][:, 0:4])
         gather_plain(2, 0, J, 8192)
-        gather_plain(3, 0, 256, 12288)
+        gather_plain(3, 0, 384, 12288)
         quantise(0)
         down(0, 0, 6)
         down(2, 0, 7)
-        gather_plain(3, 256, J, 0)
+        gather_plain(3, 384, J, 0)
         up_half(1)
         gather_add(0, 0)
         sum_half(2, 0)

@@ -1,7 +1,6 @@
 from contextlib import ExitStack
 
 import concourse.mybir as mybir
-from concourse.masks import make_identity
 
 K, R, N, T, J = 1024, 512, 512, 2048, 1024
 FLOPS = 2 * K * R * J + 2 * R * N * J
@@ -19,8 +18,8 @@ MULT = mybir.AluOpType.mult
 ADD = mybir.AluOpType.add
 
 P = 128
-HALF = J // 2
-QUARTER = J // 4
+A, B, C = (0, 256), (256, 512), (512, 1024)
+AB, ALL = (0, 512), (0, 1024)
 
 
 def tile_list_modp_relu_resb_kernel(tc, tab_words, tab_scales, wu_words, wu_scales, wd_words, wd_scales, rT, b, wgo, offs, out):
@@ -28,184 +27,186 @@ def tile_list_modp_relu_resb_kernel(tc, tab_words, tab_scales, wu_words, wu_scal
     with ExitStack() as ctx:
         keep = ctx.enter_context(tc.tile_pool(name="keep", bufs=1))
         reuse = ctx.enter_context(tc.tile_pool(name="reuse", bufs=1))
-        picks = ctx.enter_context(tc.tile_pool(name="picks", bufs=1))
-        ring = ctx.enter_context(tc.tile_pool(name="ring", bufs=2))
         psum = ctx.enter_context(tc.psum_pool(name="psum", bufs=1))
         banks = [psum.tile([P, 512], F32, name="bank%d" % i) for i in range(8)]
 
         offsets = keep.tile([P, J // 16], U16, name="offsets")
         nc.sync.dma_start(offsets[:], offs)
-        half_offsets = [offsets[:, 32 * h : 32 * h + 32] for h in range(2)]
 
-        tabs = reuse.tile([P, T], U8, name="tabs", align_bytes=64, offset=15360)
-        nc.gpsimd.memset(tabs[:, 0 : T // 2].bitcast(I32), 0)
-        nc.vector.memset(tabs[:, T // 2 : T].bitcast(I32), 0)
-        wus = keep.tile([P, 2, R], U8, name="wus", align_bytes=64)
-        brow = keep.tile([P, P], F32, name="brow", align_bytes=64)
-        nc.vector.memset(brow[:], 0.0)
-        nc.vector.memset(wus[:].bitcast(I32), 0)
-        plane1 = keep.tile([P, J], U8, name="plane1", align_bytes=64)
-        nc.vector.memset(plane1[:].bitcast(I32), 0)
+        def listed(span):
+            return offsets[:] if span == ALL else offsets[:, span[0] // 16 : span[1] // 16]
+
+        tabs = keep.tile([P, T], U8, name="tabs", align_bytes=64)
+        nc.vector.memset(tabs[:].bitcast(I32), 0)
+        wus_raw = reuse.tile([P, 2 * R], U8, name="wus_raw", align_bytes=64, offset=7680)
+        nc.vector.memset(wus_raw[:].bitcast(I32), 0)
         wds = keep.tile([P, N], U8, name="wds", align_bytes=64)
         nc.gpsimd.memset(wds[:].bitcast(I32), 0)
+        plane1 = keep.tile([P, J], U8, name="plane1", align_bytes=64)
+        nc.vector.memset(plane1[:].bitcast(I32), 0)
         for q in range(4):
             nc.gpsimd.dma_start(wds[32 * q : 32 * q + 4, :].bitcast(I32), wd_scales[0, 4 * q : 4 * q + 4, :].bitcast(I32))
-        ident = keep.tile([P, P], F32, name="ident", align_bytes=64)
-        make_identity(nc, ident[:])
+        bias = keep.tile([P, 4], F32, name="bias", align_bytes=64)
+        with nc.allow_non_contiguous_dma(reason="one bias value a partition"):
+            nc.gpsimd.dma_start(bias[:], b.rearrange("(c p) -> p c", p=P))
 
-        wu = [keep.tile([P, 2 * R], U8, name="wu%d" % a, align_bytes=64) for a in range(2)]
+        page0 = keep.tile([P, T], F32, name="page0", align_bytes=64)
+        nc.vector.memset(page0[:], 0.0)
+        wu_raw = keep.tile([P, 2, 2 * R], U8, name="wu_raw", align_bytes=64)
         tabw = [keep.tile([P, T], I32, name="tabw%d" % a, align_bytes=64) for a in range(2)]
-        res = {}
+        res = [keep.tile([P, T], F32, name="res%d" % c, align_bytes=64) for c in range(4)]
+        gate_all = keep.tile([P, J], F32, name="gate_all", align_bytes=64)
 
-        def load_res(c):
-            res[c] = keep.tile([P, T], F32, name="res%d" % c, align_bytes=64)
-            nc.sync.dma_start(res[c][:], rT[c * P : (c + 1) * P, :])
-
-        nc.sync.dma_start(wu[0][:].bitcast(I32), wu_words[0].bitcast(I32))
+        nc.sync.dma_start(wu_raw[:].bitcast(I32), wu_words.rearrange("a p w -> p a w").bitcast(I32))
         scale_rows = tab_scales.rearrange("a (q r) t -> r q a t", r=4)
         for r in range(4):
             nc.sync.dma_start(tabs[r:P:16, :].bitcast(I32), scale_rows[r].bitcast(I32))
-        nc.scalar.dma_start(brow[0:4, :], b.rearrange("(c m) -> c m", c=4))
         nc.sync.dma_start(tabw[0][:], tab_words[0].rearrange("p t i -> p (t i)").bitcast(I32))
         for q in range(4):
-            nc.sync.dma_start(wus[32 * q : 32 * q + 4, :, :].bitcast(I32), wu_scales[:, 4 * q : 4 * q + 4, :].rearrange("a r n -> r a n").bitcast(I32))
+            nc.sync.dma_start(wus_raw[32 * q : 32 * q + 4, :].rearrange("r (a n) -> r a n", a=2).bitcast(I32), wu_scales[:, 4 * q : 4 * q + 4, :].rearrange("a r n -> r a n").bitcast(I32))
         nc.sync.dma_start(tabw[1][:], tab_words[1].rearrange("p t i -> p (t i)").bitcast(I32))
-        nc.sync.dma_start(wu[1][:].bitcast(I32), wu_words[1].bitcast(I32))
 
+        wu = keep.tile([P, 4 * R], U8, name="wu", align_bytes=64)
+        nc.vector.tensor_copy(wu[:].bitcast(U16).rearrange("p (t g m) -> p g t m", t=4, m=8), wu_raw[:].rearrange("p a w -> p (a w)").bitcast(U16).rearrange("p (g m t) -> p g t m", t=4, m=8))
 
         plane0 = keep.tile([P, J], U8, name="plane0", align_bytes=64)
         nc.vector.tensor_copy(plane0[:], tabs[:].indirect(offsets[:]))
         for q in range(4):
             nc.sync.dma_start(plane1[32 * q : 32 * q + 4, :].bitcast(I32), plane0[32 * q + 16 : 32 * q + 20, :].bitcast(I32))
         planes = [plane0, plane1]
-        pages = []
-        for i in range(2):
-            page = reuse.tile([P, T], F32, name="page%d" % i, align_bytes=64, offset=8192 * (i + 1))
-            nc.gpsimd.memset(page[:], 0.0)
-            pages.append(page)
-        load_res(2)
-        load_res(3)
+
+        wus = keep.tile([P, 2 * R], U8, name="wus", align_bytes=64)
+        nc.vector.tensor_copy(wus[:].rearrange("p (t g m) -> p g t m", t=4, m=16), wus_raw[:].rearrange("p (g m t) -> p g t m", t=4, m=16))
+
         wd = keep.tile([P, N], I32, name="wd", align_bytes=64)
         nc.sync.dma_start(wd[:], wd_words[0].rearrange("p n i -> p (n i)").bitcast(I32))
-        load_res(0)
-        gate = keep.tile([P, J], F32, name="gate", align_bytes=64)
-        nc.sync.dma_start(gate[:, 0:HALF], wgo[:, 0:HALF])
-        load_res(1)
-        nc.sync.dma_start(gate[:, HALF:J], wgo[:, HALF:J])
 
+        def load_gate(span):
+            nc.sync.dma_start(gate_all[:, span[0] : span[1]], wgo[:, span[0] : span[1]])
+
+        def load_res(c):
+            nc.sync.dma_start(res[c][:], rT[c * P : (c + 1) * P, :])
+
+        load_gate(A)
+        load_res(0)
+        load_res(1)
+        load_gate(B)
+        load_res(2)
+        load_gate(C)
+        load_res(3)
 
         words = {}
-        for a in range(2):
-            for j0, j1 in ((0, QUARTER), (QUARTER, HALF), (HALF, J)):
-                wt = keep.tile([P, j1 - j0], U32, name="words%d_%d" % (a, j0), align_bytes=64)
-                nc.vector.tensor_copy(wt[:], tabw[a][:].bitcast(U32).indirect(offsets[:, j0 // 16 : j1 // 16]))
-                for j in range(j0, j1, P):
-                    words[(a, j // P)] = wt[:, j - j0 : j - j0 + P]
 
-        bias = keep.tile([P, 4], F32, name="bias", align_bytes=64)
+        def gather_words(a, span, tile):
+            nc.vector.tensor_copy(tile[:], tabw[a][:].bitcast(U32).indirect(listed(span)))
+            for j in range(span[0], span[1], P):
+                words[(a, j // P)] = tile[:, j - span[0] : j - span[0] + P]
 
-        y_sb = [keep.tile([P, J], F32, name="y%d" % c, align_bytes=64) for c in range(4)]
-        zs = {c: keep.tile([P, J], F32, name="z%d" % c, align_bytes=64)[:] for c in range(1, 4)}
-        z0 = [reuse.tile([P, HALF], F32, name="z0_%d" % h, align_bytes=64, offset=2048 * h) for h in range(2)]
-        h_t = [picks.tile([P, HALF * 4], BF16, name="hT%d" % h, align_bytes=64, offset=4096 * h) for h in range(2)]
-        picked = {}
+        up_bank = [banks[i] for i in range(8)]
 
-        def up_half(h):
-            up_banks = (banks[0:4], [banks[4], banks[6], banks[7], banks[6]])[h]
-            order = ([(a, i) for a in range(2) for i in range(4)], [(a, i) for i in range(4) for a in range(2)])[h]
-            hbs = []
-            for a, i in order:
-                pcols = slice(h * HALF + i * P, h * HALF + (i + 1) * P)
-                nc.tensor.matmul_mx(out=up_banks[i][:], lhsT=words[(a, 4 * h + i)].bitcast(FP8X4), lhsT_scale=planes[a][:, pcols],
-                                    rhs=wu[a][:].bitcast(FP4X4), rhs_scale=wus[:, a, :], start=(a == 0), stop=(a == 1))
-                if a == 1:
-                    hb = ring.tile([P, 2, P, 2], BF16, name="hb", align_bytes=64, bufs=4)
-                    nc.scalar.activation(hb[:], up_banks[i][:].rearrange("j (p u e) -> j u p e", u=2, e=2), ACT.Relu)
-                    hbs.append(hb)
-            for g in range(2):
-                xt = banks[(4, 0)[h] + g][:].rearrange("p (i u j) -> p i u j", i=2, u=2)
-                for i in range(2):
-                    hw = hbs[2 * g + i][:].rearrange("j u p e -> j (u p e)").bitcast(F32)
-                    for u in range(2):
-                        nc.tensor.transpose(xt[:, i, u, :], hw[:, u * P : (u + 1) * P], ident[:])
-                nc.scalar.copy(h_t[h][:].bitcast(F32)[:, g * 4 * P : (g + 1) * 4 * P].rearrange("p (i j u) -> p i j u", i=2, u=2), xt.rearrange("p i u j -> p i j u"))
+        def up_pass(a, i, first):
+            for t in range(4):
+                col = t * 2 * P + a * P
+                nc.tensor.matmul_mx(out=up_bank[i][:, t * P : (t + 1) * P], lhsT=wu[:, 2 * col : 2 * (col + P)].bitcast(FP4X4), lhsT_scale=wus[:, col : col + P],
+                                    rhs=words[(a, i)].bitcast(FP8X4), rhs_scale=planes[a][:, i * P : (i + 1) * P], start=(first and t == 0), stop=(not first and t == 3))
+
+        h_t = {}
+
+        def relu(span, i):
+            j = i * P - span[0]
+            nc.scalar.activation(h_t[span][:, 4 * j : 4 * (j + P)].rearrange("p (j t) -> p j t", t=4), up_bank[i][:].rearrange("p (t j) -> p j t", t=4), ACT.Relu)
 
         coded = {}
 
-        def quantise(h):
-            hq = reuse.tile([P, HALF], U32, name="hq%d" % h, align_bytes=64, offset=(4096, 0)[h])
-            hs = ring.tile([P, HALF], U8, name="hs", align_bytes=64)
-            nc.vector.quantize_mx(out=hq[:].bitcast(FP8X4), scales=hs[:], in_=h_t[h][:])
-            coded[h] = (hq, hs)
+        def quantise(span, offset):
+            n = span[1] - span[0]
+            hq = reuse.tile([P, n], U32, name="hq%d" % span[0], align_bytes=64, offset=offset)
+            hs = keep.tile([P, n], U8, name="hs%d" % span[0], align_bytes=64)
+            nc.vector.quantize_mx(out=hq[:].bitcast(FP8X4), scales=hs[:], in_=h_t[span][:])
+            coded[span] = (hq, hs)
 
-        def down(c, h, bank):
-            hq, hs = coded[h]
-            nc.tensor.matmul_mx(out=banks[bank][:], lhsT=wd[:, c * P : (c + 1) * P].bitcast(FP8X4), lhsT_scale=wds[:, c * P : (c + 1) * P],
-                                rhs=hq[:].bitcast(FP8X4), rhs_scale=hs[:], start=True, stop=True)
-            nc.scalar.activation(y_sb[c][:, h * HALF : (h + 1) * HALF], banks[bank][:], ACT.Identity, bias=bias[:, c : c + 1])
+        def down(c, spans, bank, y):
+            at = 0
+            for span in spans:
+                hq, hs = coded[span]
+                n = span[1] - span[0]
+                nc.tensor.matmul_mx(out=banks[bank][:, at : at + n], lhsT=wd[:, c * P : (c + 1) * P].bitcast(FP8X4), lhsT_scale=wds[:, c * P : (c + 1) * P],
+                                    rhs=hq[:].bitcast(FP8X4), rhs_scale=hs[:], start=True, stop=True)
+                at += n
+            nc.scalar.activation(y, banks[bank][:, 0:at], ACT.Identity, bias=bias[:, c : c + 1])
 
-        def span(h):
-            return (offsets[:], slice(0, J)) if h is None else (half_offsets[h], slice(h * HALF, (h + 1) * HALF))
+        zs = {}
 
-        def gather_add(c, h):
-            lst, cols = span(h)
-            nc.vector.tensor_tensor(z0[h][:] if c == 0 else zs[c][:, cols], res[c][:].indirect(lst), y_sb[c][:, cols], ADD)
+        def gather_add(c, span, y, z=None):
+            if z is None:
+                z = keep.tile([P, span[1] - span[0]], F32, name="z%d_%d" % (c, span[0]), align_bytes=64)
+            nc.vector.tensor_tensor(z[:], res[c][:].indirect(listed(span)), y, ADD)
+            zs[(c, span)] = z
 
-        def gather_plain(c, j0, j1, offset):
-            rg = picks.tile([P, j1 - j0], F32, name="rg%d_%d" % (c, j0), align_bytes=64, offset=offset)
-            nc.vector.tensor_copy(rg[:], res[c][:].indirect(offsets[:, j0 // 16 : j1 // 16]))
-            for j in range(j0, j1, P):
-                picked[(c, j // P)] = rg[:, j - j0 : j - j0 + P]
+        def scatter(c, span, page):
+            nc.vector.tensor_tensor(page[:].indirect(listed(span)), zs[(c, span)][:], gate_all[:, span[0] : span[1]], MULT)
 
-        def sum_half(c, h):
-            across = banks[(3, 2 * (c % 2))[h]]
-            for i in range(4):
-                nc.tensor.matmul(across[:, i * P : (i + 1) * P], picked[(c, 4 * h + i)], ident[:], start=(i == 0), stop=False, is_transpose=True)
-            for i in range(4):
-                nc.tensor.matmul(across[:, i * P : (i + 1) * P], y_sb[c][:, h * HALF + i * P : h * HALF + (i + 1) * P], ident[:], start=False, stop=(i == 3), is_transpose=True)
-            turned = ring.tile([P, HALF], F32, name="turned", align_bytes=64)
-            nc.scalar.copy(turned[:], across[:])
-            back = banks[(2, 2 * (c % 2) + 1)[h]]
-            for i in range(4):
-                nc.tensor.transpose(back[:, i * P : (i + 1) * P], turned[:, i * P : (i + 1) * P], ident[:])
-            nc.scalar.copy(zs[c][:, h * HALF : (h + 1) * HALF], back[:])
+        def store(c, page):
+            nc.sync.dma_start(out[c * P : (c + 1) * P, :], page[:])
 
-        def scatter(c, h):
-            lst, cols = span(h)
-            nc.vector.tensor_tensor(pages[c // 2][:].indirect(lst), z0[h][:] if c == 0 else zs[c][:, cols], gate[:, cols], MULT)
-
-        def store(c):
-            nc.sync.dma_start(out[c * P : (c + 1) * P, :], pages[c // 2][:])
-
-        up_half(0)
-        nc.tensor.transpose(banks[2][:, 0:P], brow[:], ident[:])
-        nc.scalar.copy(bias[:], banks[2][:, 0:4])
-        gather_plain(2, 0, J, 8192)
-        gather_plain(3, 0, 384, 12288)
-        quantise(0)
-        down(0, 0, 6)
-        down(2, 0, 7)
-        gather_plain(3, 384, J, 0)
-        up_half(1)
-        gather_add(0, 0)
-        sum_half(2, 0)
-        scatter(0, 0)
-        down(1, 0, 5)
-        down(3, 0, 7)
-        sum_half(3, 0)
-        quantise(1)
-        for c in (0, 2, 1, 3):
-            down(c, 1, 4 + c)
-        scatter(2, 0)
-        gather_add(0, 1)
-        gather_add(1, 0)
-        sum_half(2, 1)
-        scatter(0, 1)
-        store(0)
-        gather_add(1, 1)
-        sum_half(3, 1)
-        scatter(2, 1)
-        store(2)
-        for c in (1, 3):
-            scatter(c, None)
-            store(c)
+        gather_words(0, A, reuse.tile([P, 256], U32, name="w0a", align_bytes=64, offset=8192))
+        gather_words(1, A, reuse.tile([P, 256], U32, name="w1a", align_bytes=64, offset=16384))
+        gather_words(1, B, keep.tile([P, 256], U32, name="w1b", align_bytes=64))
+        gather_words(1, C, keep.tile([P, 512], U32, name="w1c", align_bytes=64))
+        h_t[A] = reuse.tile([P, 1024], BF16, name="hA", align_bytes=64, offset=10752)
+        h_t[C] = keep.tile([P, 2048], BF16, name="hC", align_bytes=64)
+        for i in range(2):
+            up_pass(0, i, True)
+        for i in range(2):
+            up_pass(1, i, False)
+            relu(A, i)
+        for i in range(2, 4):
+            up_pass(1, i, True)
+        gather_words(0, B, reuse.tile([P, 256], U32, name="w0b", align_bytes=64, offset=16384))
+        quantise(A, 17408)
+        h_t[B] = reuse.tile([P, 1024], BF16, name="hB", align_bytes=64, offset=9216)
+        up_pass(0, 2, False)
+        relu(B, 2)
+        y0a = reuse.tile([P, 256], F32, name="y0a", align_bytes=64, offset=13312)
+        down(0, [A], 0, y0a[:])
+        up_pass(0, 3, False)
+        relu(B, 3)
+        gather_words(0, C, reuse.tile([P, 512], U32, name="w0c", align_bytes=64, offset=11264))
+        gather_add(0, A, y0a[:], reuse.tile([P, 256], F32, name="z0a", align_bytes=64, offset=14336))
+        quantise(B, 13312)
+        page1 = reuse.tile([P, T], F32, name="page1", align_bytes=64, offset=0)
+        nc.gpsimd.memset(page1[:], 0.0)
+        scatter(0, A, page0)
+        for i in range(4, 8):
+            up_pass(0, i, True)
+            up_pass(1, i, False)
+            relu(C, i)
+        y1ab = keep.tile([P, 512], F32, name="y1ab", align_bytes=64)
+        down(1, [A, B], 2, y1ab[:])
+        y0b = keep.tile([P, 256], F32, name="y0b", align_bytes=64)
+        down(0, [B], 1, y0b[:])
+        quantise(C, 14336)
+        y23 = {c: keep.tile([P, J], F32, name="y%d" % c, align_bytes=64) for c in (2, 3)}
+        gather_add(1, AB, y1ab[:])
+        gather_add(0, B, y0b[:])
+        scatter(1, AB, page1)
+        scatter(0, B, page0)
+        y0c = keep.tile([P, 512], F32, name="y0c", align_bytes=64)
+        down(0, [C], 0, y0c[:])
+        y1c = keep.tile([P, 512], F32, name="y1c", align_bytes=64)
+        down(1, [C], 3, y1c[:])
+        for c in (2, 3):
+            down(c, [A, B], 3 * c - 6, y23[c][:, 0:512])
+            down(c, [C], c + 2, y23[c][:, 512:1024])
+        gather_add(0, C, y0c[:])
+        gather_add(1, C, y1c[:])
+        gather_add(2, ALL, y23[2][:])
+        scatter(0, C, page0)
+        store(0, page0)
+        scatter(1, C, page1)
+        store(1, page1)
+        gather_add(3, ALL, y23[3][:])
+        scatter(2, ALL, page0)
+        store(2, page0)
+        scatter(3, ALL, page1)
+        store(3, page1)

@@ -1,6 +1,7 @@
 from contextlib import ExitStack
 
 import concourse.mybir as mybir
+from concourse.masks import make_identity
 
 K, R, N, T, J = 1024, 512, 512, 2048, 1024
 FLOPS = 2 * K * R * J + 2 * R * N * J
@@ -19,7 +20,7 @@ ADD = mybir.AluOpType.add
 
 P = 128
 A, B, C = (0, 256), (256, 512), (512, 1024)
-AB, ALL = (0, 512), (0, 1024)
+AB, BC, ALL = (0, 512), (256, 1024), (0, 1024)
 
 
 def tile_list_modp_relu_resb_kernel(tc, tab_words, tab_scales, wu_words, wu_scales, wd_words, wd_scales, rT, b, wgo, offs, out):
@@ -38,7 +39,7 @@ def tile_list_modp_relu_resb_kernel(tc, tab_words, tab_scales, wu_words, wu_scal
 
         tabs = keep.tile([P, T], U8, name="tabs", align_bytes=64)
         nc.vector.memset(tabs[:].bitcast(I32), 0)
-        wus_raw = reuse.tile([P, 2 * R], U8, name="wus_raw", align_bytes=64, offset=7680)
+        wus_raw = reuse.tile([P, 2 * R], U8, name="wus_raw", align_bytes=64, offset=26112)
         nc.vector.memset(wus_raw[:].bitcast(I32), 0)
         wds = keep.tile([P, N], U8, name="wds", align_bytes=64)
         nc.gpsimd.memset(wds[:].bitcast(I32), 0)
@@ -47,8 +48,6 @@ def tile_list_modp_relu_resb_kernel(tc, tab_words, tab_scales, wu_words, wu_scal
         for q in range(4):
             nc.gpsimd.dma_start(wds[32 * q : 32 * q + 4, :].bitcast(I32), wd_scales[0, 4 * q : 4 * q + 4, :].bitcast(I32))
         bias = keep.tile([P, 4], F32, name="bias", align_bytes=64)
-        with nc.allow_non_contiguous_dma(reason="one bias value a partition"):
-            nc.gpsimd.dma_start(bias[:], b.rearrange("(c p) -> p c", p=P))
 
         page0 = keep.tile([P, T], F32, name="page0", align_bytes=64)
         nc.vector.memset(page0[:], 0.0)
@@ -76,10 +75,11 @@ def tile_list_modp_relu_resb_kernel(tc, tab_words, tab_scales, wu_words, wu_scal
         planes = [plane0, plane1]
 
         wus = keep.tile([P, 2 * R], U8, name="wus", align_bytes=64)
-        nc.vector.tensor_copy(wus[:].rearrange("p (t g m) -> p g t m", t=4, m=16), wus_raw[:].rearrange("p (g m t) -> p g t m", t=4, m=16))
+        nc.gpsimd.tensor_copy(wus[:].rearrange("p (t m) -> p t m", t=4), wus_raw[:].rearrange("p (m t) -> p t m", t=4))
 
+        ident = reuse.tile([P, P], F32, name="ident", align_bytes=64, offset=26112)
+        make_identity(nc, ident[:])
         wd = keep.tile([P, N], I32, name="wd", align_bytes=64)
-        nc.sync.dma_start(wd[:], wd_words[0].rearrange("p n i -> p (n i)").bitcast(I32))
 
         def load_gate(span):
             nc.sync.dma_start(gate_all[:, span[0] : span[1]], wgo[:, span[0] : span[1]])
@@ -87,8 +87,11 @@ def tile_list_modp_relu_resb_kernel(tc, tab_words, tab_scales, wu_words, wu_scal
         def load_res(c):
             nc.sync.dma_start(res[c][:], rT[c * P : (c + 1) * P, :])
 
-        load_gate(A)
         load_res(0)
+        nc.sync.dma_start(wd[:], wd_words[0].rearrange("p n i -> p (n i)").bitcast(I32))
+        with nc.allow_non_contiguous_dma(reason="one bias value a partition"):
+            nc.sync.dma_start(bias[:], b.rearrange("(c p) -> p c", p=P))
+        load_gate(A)
         load_res(1)
         load_gate(B)
         load_res(2)
@@ -102,7 +105,7 @@ def tile_list_modp_relu_resb_kernel(tc, tab_words, tab_scales, wu_words, wu_scal
             for j in range(span[0], span[1], P):
                 words[(a, j // P)] = tile[:, j - span[0] : j - span[0] + P]
 
-        up_bank = [banks[i] for i in range(8)]
+        up_bank = [banks[i] for i in (0, 1, 2, 3, 2, 3, 0, 2)]
 
         def up_pass(a, i, first):
             for t in range(4):
@@ -149,7 +152,20 @@ def tile_list_modp_relu_resb_kernel(tc, tab_words, tab_scales, wu_words, wu_scal
         def store(c, page):
             nc.sync.dma_start(out[c * P : (c + 1) * P, :], page[:])
 
-        gather_words(0, A, reuse.tile([P, 256], U32, name="w0a", align_bytes=64, offset=8192))
+        def sum_turned(c, span, picked, y, z, across, back):
+            n = (span[1] - span[0]) // P
+            for i in range(n):
+                nc.tensor.matmul(banks[across][:, i * P : (i + 1) * P], picked[:, i * P : (i + 1) * P], ident[:], start=(i == 0), stop=False, is_transpose=True)
+            for i in range(n):
+                nc.tensor.matmul(banks[across][:, i * P : (i + 1) * P], y[:, i * P : (i + 1) * P], ident[:], start=False, stop=(i == n - 1), is_transpose=True)
+            turned = keep.tile([P, n * P], F32, name="turned%d" % span[0], align_bytes=64)
+            nc.scalar.copy(turned[:], banks[across][:, 0 : n * P])
+            for i in range(n):
+                nc.tensor.transpose(banks[back][:, i * P : (i + 1) * P], turned[:, i * P : (i + 1) * P], ident[:])
+            nc.scalar.copy(z, banks[back][:, 0 : n * P])
+
+        gather_words(0, A, keep.tile([P, 256], U32, name="w0a", align_bytes=64))
+        gather_words(0, (256, 768), keep.tile([P, 512], U32, name="w0b", align_bytes=64))
         gather_words(1, A, reuse.tile([P, 256], U32, name="w1a", align_bytes=64, offset=16384))
         gather_words(1, B, keep.tile([P, 256], U32, name="w1b", align_bytes=64))
         gather_words(1, C, keep.tile([P, 512], U32, name="w1c", align_bytes=64))
@@ -160,51 +176,55 @@ def tile_list_modp_relu_resb_kernel(tc, tab_words, tab_scales, wu_words, wu_scal
         for i in range(2):
             up_pass(1, i, False)
             relu(A, i)
-        for i in range(2, 4):
-            up_pass(1, i, True)
-        gather_words(0, B, reuse.tile([P, 256], U32, name="w0b", align_bytes=64, offset=16384))
+        gather_words(0, (768, 1024), reuse.tile([P, 256], U32, name="w0c", align_bytes=64, offset=16384))
+        picked_b = keep.tile([P, 256], F32, name="picked_b", align_bytes=64)
+        nc.vector.tensor_copy(picked_b[:], res[0][:].indirect(listed(B)))
         quantise(A, 17408)
-        h_t[B] = reuse.tile([P, 1024], BF16, name="hB", align_bytes=64, offset=9216)
+        h_t[B] = reuse.tile([P, 1024], BF16, name="hB", align_bytes=64, offset=6144)
+        up_pass(1, 2, True)
         up_pass(0, 2, False)
         relu(B, 2)
-        y0a = reuse.tile([P, 256], F32, name="y0a", align_bytes=64, offset=13312)
+        y0a = keep.tile([P, 256], F32, name="y0a", align_bytes=64)
         down(0, [A], 0, y0a[:])
+        up_pass(1, 3, True)
         up_pass(0, 3, False)
         relu(B, 3)
-        gather_words(0, C, reuse.tile([P, 512], U32, name="w0c", align_bytes=64, offset=11264))
-        gather_add(0, A, y0a[:], reuse.tile([P, 256], F32, name="z0a", align_bytes=64, offset=14336))
+        picked_c = reuse.tile([P, 512], F32, name="picked_c", align_bytes=64, offset=10752)
+        nc.vector.tensor_copy(picked_c[:], res[0][:].indirect(listed(C)))
+        gather_add(0, A, y0a[:])
         quantise(B, 13312)
-        page1 = reuse.tile([P, T], F32, name="page1", align_bytes=64, offset=0)
+        page1 = reuse.tile([P, T], F32, name="page1", align_bytes=64, offset=26624)
         nc.gpsimd.memset(page1[:], 0.0)
         scatter(0, A, page0)
-        for i in range(4, 8):
-            up_pass(0, i, True)
-            up_pass(1, i, False)
-            relu(C, i)
         y1ab = keep.tile([P, 512], F32, name="y1ab", align_bytes=64)
-        down(1, [A, B], 2, y1ab[:])
-        y0b = keep.tile([P, 256], F32, name="y0b", align_bytes=64)
-        down(0, [B], 1, y0b[:])
-        quantise(C, 14336)
-        y23 = {c: keep.tile([P, J], F32, name="y%d" % c, align_bytes=64) for c in (2, 3)}
+        for i in range(4, 8):
+            up_pass(1, i, True)
+            up_pass(0, i, False)
+            if i == 7:
+                down(1, [A, B], 3, y1ab[:])
+            relu(C, i)
         gather_add(1, AB, y1ab[:])
-        gather_add(0, B, y0b[:])
+        quantise(C, 14336)
         scatter(1, AB, page1)
-        scatter(0, B, page0)
-        y0c = keep.tile([P, 512], F32, name="y0c", align_bytes=64)
-        down(0, [C], 0, y0c[:])
+        y0bc = keep.tile([P, 768], F32, name="y0bc", align_bytes=64)
+        z0bc = keep.tile([P, 768], F32, name="z0bc", align_bytes=64)
+        zs[(0, BC)] = z0bc
         y1c = keep.tile([P, 512], F32, name="y1c", align_bytes=64)
-        down(1, [C], 3, y1c[:])
+        down(1, [C], 4, y1c[:])
+        down(0, [B], 7, y0bc[:, 0:256])
+        sum_turned(0, B, picked_b[:], y0bc[:, 0:256], z0bc[:, 0:256], 6, 1)
+        down(0, [C], 5, y0bc[:, 256:768])
+        sum_turned(0, C, picked_c[:], y0bc[:, 256:768], z0bc[:, 256:768], 0, 2)
+        y23 = {c: keep.tile([P, J], F32, name="y%d" % c, align_bytes=64) for c in (2, 3)}
         for c in (2, 3):
-            down(c, [A, B], 3 * c - 6, y23[c][:, 0:512])
-            down(c, [C], c + 2, y23[c][:, 512:1024])
-        gather_add(0, C, y0c[:])
+            down(c, [A, B], 4, y23[c][:, 0:512])
+            down(c, [C], 5, y23[c][:, 512:1024])
         gather_add(1, C, y1c[:])
-        gather_add(2, ALL, y23[2][:])
-        scatter(0, C, page0)
+        scatter(0, BC, page0)
         store(0, page0)
         scatter(1, C, page1)
         store(1, page1)
+        gather_add(2, ALL, y23[2][:])
         gather_add(3, ALL, y23[3][:])
         scatter(2, ALL, page0)
         store(2, page0)

@@ -75,7 +75,8 @@ def tile_list_modp_relu_resb_kernel(tc, tab_words, tab_scales, wu_words, wu_scal
         planes = [plane0, plane1]
 
         wus = keep.tile([P, 2 * R], U8, name="wus", align_bytes=64)
-        nc.gpsimd.tensor_copy(wus[:].rearrange("p (t m) -> p t m", t=4), wus_raw[:].rearrange("p (m t) -> p t m", t=4))
+        for a in range(2):
+            nc.gpsimd.tensor_copy(wus[:].rearrange("p (t a m) -> p a t m", t=4, a=2)[:, a], wus_raw[:].rearrange("p (a m t) -> p a t m", t=4, a=2)[:, a])
 
         ident = reuse.tile([P, P], F32, name="ident", align_bytes=64, offset=26112)
         make_identity(nc, ident[:])
@@ -105,7 +106,7 @@ def tile_list_modp_relu_resb_kernel(tc, tab_words, tab_scales, wu_words, wu_scal
             for j in range(span[0], span[1], P):
                 words[(a, j // P)] = tile[:, j - span[0] : j - span[0] + P]
 
-        up_bank = [banks[i] for i in (0, 1, 2, 3, 2, 3, 0, 2)]
+        up_bank = [banks[i] for i in (0, 1, 2, 3, 4, 3, 0, 4)]
 
         def up_pass(a, i, first):
             for t in range(4):
@@ -142,8 +143,8 @@ def tile_list_modp_relu_resb_kernel(tc, tab_words, tab_scales, wu_words, wu_scal
 
         def gather_add(c, span, y, z=None):
             if z is None:
-                z = keep.tile([P, span[1] - span[0]], F32, name="z%d_%d" % (c, span[0]), align_bytes=64)
-            nc.vector.tensor_tensor(z[:], res[c][:].indirect(listed(span)), y, ADD)
+                z = keep.tile([P, span[1] - span[0]], F32, name="z%d_%d" % (c, span[0]), align_bytes=64)[:]
+            nc.vector.tensor_tensor(z, res[c][:].indirect(listed(span)), y, ADD)
             zs[(c, span)] = z
 
         def scatter(c, span, page):
@@ -152,7 +153,7 @@ def tile_list_modp_relu_resb_kernel(tc, tab_words, tab_scales, wu_words, wu_scal
         def store(c, page):
             nc.sync.dma_start(out[c * P : (c + 1) * P, :], page[:])
 
-        def sum_turned(c, span, picked, y, z, across, back):
+        def sum_across(span, picked, y, across):
             n = (span[1] - span[0]) // P
             for i in range(n):
                 nc.tensor.matmul(banks[across][:, i * P : (i + 1) * P], picked[:, i * P : (i + 1) * P], ident[:], start=(i == 0), stop=False, is_transpose=True)
@@ -160,34 +161,34 @@ def tile_list_modp_relu_resb_kernel(tc, tab_words, tab_scales, wu_words, wu_scal
                 nc.tensor.matmul(banks[across][:, i * P : (i + 1) * P], y[:, i * P : (i + 1) * P], ident[:], start=False, stop=(i == n - 1), is_transpose=True)
             turned = keep.tile([P, n * P], F32, name="turned%d" % span[0], align_bytes=64)
             nc.scalar.copy(turned[:], banks[across][:, 0 : n * P])
+            return turned
+
+        def turn_back(span, turned, back, z):
+            n = (span[1] - span[0]) // P
             for i in range(n):
                 nc.tensor.transpose(banks[back][:, i * P : (i + 1) * P], turned[:, i * P : (i + 1) * P], ident[:])
             nc.scalar.copy(z, banks[back][:, 0 : n * P])
 
-        gather_words(0, A, keep.tile([P, 256], U32, name="w0a", align_bytes=64))
-        gather_words(0, (256, 768), keep.tile([P, 512], U32, name="w0b", align_bytes=64))
-        gather_words(1, A, reuse.tile([P, 256], U32, name="w1a", align_bytes=64, offset=16384))
-        gather_words(1, B, keep.tile([P, 256], U32, name="w1b", align_bytes=64))
-        gather_words(1, C, keep.tile([P, 512], U32, name="w1c", align_bytes=64))
+        gather_words(0, AB, keep.tile([P, 512], U32, name="w0ab", align_bytes=64))
+        gather_words(0, C, reuse.tile([P, 512], U32, name="w0c", align_bytes=64, offset=36864))
+        gather_words(1, A, keep.tile([P, 256], U32, name="w1a", align_bytes=64))
+        gather_words(1, BC, keep.tile([P, 768], U32, name="w1bc", align_bytes=64))
         h_t[A] = reuse.tile([P, 1024], BF16, name="hA", align_bytes=64, offset=10752)
         h_t[C] = keep.tile([P, 2048], BF16, name="hC", align_bytes=64)
-        for i in range(2):
+        for i in range(4):
             up_pass(0, i, True)
         for i in range(2):
             up_pass(1, i, False)
             relu(A, i)
-        gather_words(0, (768, 1024), reuse.tile([P, 256], U32, name="w0c", align_bytes=64, offset=16384))
         picked_b = keep.tile([P, 256], F32, name="picked_b", align_bytes=64)
         nc.vector.tensor_copy(picked_b[:], res[0][:].indirect(listed(B)))
         quantise(A, 17408)
         h_t[B] = reuse.tile([P, 1024], BF16, name="hB", align_bytes=64, offset=6144)
-        up_pass(1, 2, True)
-        up_pass(0, 2, False)
+        up_pass(1, 2, False)
         relu(B, 2)
         y0a = keep.tile([P, 256], F32, name="y0a", align_bytes=64)
         down(0, [A], 0, y0a[:])
-        up_pass(1, 3, True)
-        up_pass(0, 3, False)
+        up_pass(1, 3, False)
         relu(B, 3)
         picked_c = reuse.tile([P, 512], F32, name="picked_c", align_bytes=64, offset=10752)
         nc.vector.tensor_copy(picked_c[:], res[0][:].indirect(listed(C)))
@@ -196,37 +197,36 @@ def tile_list_modp_relu_resb_kernel(tc, tab_words, tab_scales, wu_words, wu_scal
         page1 = reuse.tile([P, T], F32, name="page1", align_bytes=64, offset=26624)
         nc.gpsimd.memset(page1[:], 0.0)
         scatter(0, A, page0)
-        y1ab = keep.tile([P, 512], F32, name="y1ab", align_bytes=64)
+        y = {(c, span): keep.tile([P, span[1] - span[0]], F32, name="y%d_%d" % (c, span[0]), align_bytes=64) for c, span in ((0, B), (0, C), (1, C), (2, ALL), (3, ALL))}
         for i in range(4, 8):
             up_pass(1, i, True)
             up_pass(0, i, False)
-            if i == 7:
-                down(1, [A, B], 3, y1ab[:])
             relu(C, i)
-        gather_add(1, AB, y1ab[:])
         quantise(C, 14336)
-        scatter(1, AB, page1)
-        y0bc = keep.tile([P, 768], F32, name="y0bc", align_bytes=64)
-        z0bc = keep.tile([P, 768], F32, name="z0bc", align_bytes=64)
-        zs[(0, BC)] = z0bc
-        y1c = keep.tile([P, 512], F32, name="y1c", align_bytes=64)
-        down(1, [C], 4, y1c[:])
-        down(0, [B], 7, y0bc[:, 0:256])
-        sum_turned(0, B, picked_b[:], y0bc[:, 0:256], z0bc[:, 0:256], 6, 1)
-        down(0, [C], 5, y0bc[:, 256:768])
-        sum_turned(0, C, picked_c[:], y0bc[:, 256:768], z0bc[:, 256:768], 0, 2)
-        y23 = {c: keep.tile([P, J], F32, name="y%d" % c, align_bytes=64) for c in (2, 3)}
-        for c in (2, 3):
-            down(c, [A, B], 4, y23[c][:, 0:512])
-            down(c, [C], 5, y23[c][:, 512:1024])
-        gather_add(1, C, y1c[:])
+        y[(1, AB)] = reuse.tile([P, 512], F32, name="y1_0", align_bytes=64, offset=36864)
+        down(1, [A, B], 1, y[(1, AB)][:])
+        down(1, [C], 5, y[(1, C)][:])
+        down(0, [B], 2, y[(0, B)][:])
+        down(0, [C], 6, y[(0, C)][:])
+        z0 = keep.tile([P, 768], F32, name="z0", align_bytes=64)
+        z1 = keep.tile([P, J], F32, name="z1", align_bytes=64)
+        zs[(0, BC)] = z0
+        gather_add(1, AB, y[(1, AB)][:], z1[:, 0:512])
+        gather_add(1, C, y[(1, C)][:], z1[:, 512:1024])
+        zs[(1, ALL)] = z1
+        scatter(1, ALL, page1)
+        store(1, page1)
+        turned_b = sum_across(B, picked_b[:], y[(0, B)][:], 4)
+        turned_c = sum_across(C, picked_c[:], y[(0, C)][:], 7)
+        turn_back(B, turned_b, 3, z0[:, 0:256])
+        turn_back(C, turned_c, 2, z0[:, 256:768])
         scatter(0, BC, page0)
         store(0, page0)
-        scatter(1, C, page1)
-        store(1, page1)
-        gather_add(2, ALL, y23[2][:])
-        gather_add(3, ALL, y23[3][:])
-        scatter(2, ALL, page0)
-        store(2, page0)
-        scatter(3, ALL, page1)
-        store(3, page1)
+        for c in (2, 3):
+            down(c, [A, B], 0, y[(c, ALL)][:, 0:512])
+            down(c, [C], 5, y[(c, ALL)][:, 512:1024])
+            gather_add(c, ALL, y[(c, ALL)][:])
+        scatter(2, ALL, page1)
+        store(2, page1)
+        scatter(3, ALL, page0)
+        store(3, page0)

@@ -74,6 +74,9 @@ def tile_list_modp_relu_resb_kernel(tc, tab_words, tab_scales, wu_words, wu_scal
             nc.sync.dma_start(plane1[32 * q : 32 * q + 4, :].bitcast(I32), plane0[32 * q + 16 : 32 * q + 20, :].bitcast(I32))
         planes = [plane0, plane1]
 
+        for n in range(2):
+            nc.tensor.matmul_mx(out=banks[7][:], lhsT=tabw[0][:, n * P : (n + 1) * P].bitcast(FP8X4), lhsT_scale=tabs[:, n * P : (n + 1) * P],
+                                rhs=wu_raw[:, 0, :].bitcast(FP4X4), rhs_scale=wus_raw[:, 0:R], start=True, stop=True)
         wus = keep.tile([P, 2 * R], U8, name="wus", align_bytes=64)
         for a in range(2):
             nc.gpsimd.tensor_copy(wus[:].rearrange("p (t a m) -> p a t m", t=4, a=2)[:, a], wus_raw[:].rearrange("p (a m t) -> p a t m", t=4, a=2)[:, a])
@@ -229,4 +232,5 @@ def tile_list_modp_relu_resb_kernel(tc, tab_words, tab_scales, wu_words, wu_scal
         scatter(2, ALL, page1)
         store(2, page1)
         scatter(3, ALL, page0)
-        store(3, page0)
+        for n, queue in enumerate((nc.sync, nc.scalar)):
+            queue.dma_start(out[3 * P : 4 * P, n * J : (n + 1) * J], page0[:, n * J : (n + 1) * J])

@@ -97,9 +97,8 @@ def tile_list_modp_relu_resb_kernel(tc, tab_words, tab_scales, wu_words, wu_scal
             nc.sync.dma_start(bias[:], b.rearrange("(c p) -> p c", p=P))
         load_gate(A)
         load_res(1)
-        load_gate(B)
         load_res(2)
-        load_gate(C)
+        load_gate(BC)
         load_res(3)
 
         words = {}
@@ -208,14 +207,20 @@ def tile_list_modp_relu_resb_kernel(tc, tab_words, tab_scales, wu_words, wu_scal
         quantise(C, 14336)
         y[(1, AB)] = reuse.tile([P, 512], F32, name="y1_0", align_bytes=64, offset=36864)
         down(1, [A, B], 1, y[(1, AB)][:])
+        down(2, [A, B], 1, y[(2, ALL)][:, 0:512])
         down(1, [C], 5, y[(1, C)][:])
-        down(0, [B], 2, y[(0, B)][:])
+        down(2, [C], 6, y[(2, ALL)][:, 512:1024])
+        down(0, [B], 5, y[(0, B)][:])
         down(0, [C], 6, y[(0, C)][:])
         z0 = keep.tile([P, 768], F32, name="z0", align_bytes=64)
         z1 = keep.tile([P, J], F32, name="z1", align_bytes=64)
         zs[(0, BC)] = z0
         gather_add(1, AB, y[(1, AB)][:], z1[:, 0:512])
+        z2 = keep.tile([P, J], F32, name="z2", align_bytes=64)
+        zs[(2, ALL)] = z2
+        gather_add(2, AB, y[(2, ALL)][:, 0:512], z2[:, 0:512])
         gather_add(1, C, y[(1, C)][:], z1[:, 512:1024])
+        gather_add(2, C, y[(2, ALL)][:, 512:1024], z2[:, 512:1024])
         zs[(1, ALL)] = z1
         scatter(1, ALL, page1)
         store(1, page1)
@@ -225,10 +230,9 @@ def tile_list_modp_relu_resb_kernel(tc, tab_words, tab_scales, wu_words, wu_scal
         turn_back(C, turned_c, 2, z0[:, 256:768])
         scatter(0, BC, page0)
         store(0, page0)
-        for c in (2, 3):
-            down(c, [A, B], 0, y[(c, ALL)][:, 0:512])
-            down(c, [C], 5, y[(c, ALL)][:, 512:1024])
-            gather_add(c, ALL, y[(c, ALL)][:])
+        down(3, [A, B], 5, y[(3, ALL)][:, 0:512])
+        down(3, [C], 6, y[(3, ALL)][:, 512:1024])
+        gather_add(3, ALL, y[(3, ALL)][:])
         scatter(2, ALL, page1)
         store(2, page1)
         scatter(3, ALL, page0)

@@ -42,9 +42,7 @@ def tile_list_modp_relu_resb_kernel(tc, tab_words, tab_scales, wu_words, wu_scal
         wus_raw = reuse.tile([P, 2 * R], U8, name="wus_raw", align_bytes=64, offset=26112)
         nc.vector.memset(wus_raw[:].bitcast(I32), 0)
         wds = keep.tile([P, N], U8, name="wds", align_bytes=64)
-        nc.gpsimd.memset(wds[:].bitcast(I32), 0)
         plane1 = keep.tile([P, J], U8, name="plane1", align_bytes=64)
-        nc.vector.memset(plane1[:].bitcast(I32), 0)
         for q in range(4):
             nc.gpsimd.dma_start(wds[32 * q : 32 * q + 4, :].bitcast(I32), wd_scales[0, 4 * q : 4 * q + 4, :].bitcast(I32))
         bias = keep.tile([P, 4], F32, name="bias", align_bytes=64)
@@ -92,11 +90,11 @@ def tile_list_modp_relu_resb_kernel(tc, tab_words, tab_scales, wu_words, wu_scal
             nc.sync.dma_start(res[c][:], rT[c * P : (c + 1) * P, :])
 
         load_res(0)
+        load_res(1)
         nc.sync.dma_start(wd[:], wd_words[0].rearrange("p n i -> p (n i)").bitcast(I32))
         with nc.allow_non_contiguous_dma(reason="one bias value a partition"):
             nc.sync.dma_start(bias[:], b.rearrange("(c p) -> p c", p=P))
         load_gate(A)
-        load_res(1)
         load_res(2)
         load_gate(BC)
         load_res(3)
@@ -108,7 +106,7 @@ def tile_list_modp_relu_resb_kernel(tc, tab_words, tab_scales, wu_words, wu_scal
             for j in range(span[0], span[1], P):
                 words[(a, j // P)] = tile[:, j - span[0] : j - span[0] + P]
 
-        up_bank = [banks[i] for i in (0, 1, 2, 3, 4, 3, 0, 4)]
+        up_bank = [banks[i] for i in (0, 1, 2, 3, 4, 5, 6, 0)]
 
         def up_pass(a, i, first):
             for t in range(4):
@@ -124,9 +122,9 @@ def tile_list_modp_relu_resb_kernel(tc, tab_words, tab_scales, wu_words, wu_scal
 
         coded = {}
 
-        def quantise(span, offset):
+        def quantise(span):
             n = span[1] - span[0]
-            hq = reuse.tile([P, n], U32, name="hq%d" % span[0], align_bytes=64, offset=offset)
+            hq = keep.tile([P, n], U32, name="hq%d" % span[0], align_bytes=64)
             hs = keep.tile([P, n], U8, name="hs%d" % span[0], align_bytes=64)
             nc.vector.quantize_mx(out=hq[:].bitcast(FP8X4), scales=hs[:], in_=h_t[span][:])
             coded[span] = (hq, hs)
@@ -134,10 +132,11 @@ def tile_list_modp_relu_resb_kernel(tc, tab_words, tab_scales, wu_words, wu_scal
         def down(c, spans, bank, y):
             at = 0
             for span in spans:
-                hq, hs = coded[span]
+                half = AB if span[1] <= AB[1] else C
+                hq, hs = (t[:, span[0] - half[0] : span[1] - half[0]] for t in coded[half])
                 n = span[1] - span[0]
                 nc.tensor.matmul_mx(out=banks[bank][:, at : at + n], lhsT=wd[:, c * P : (c + 1) * P].bitcast(FP8X4), lhsT_scale=wds[:, c * P : (c + 1) * P],
-                                    rhs=hq[:].bitcast(FP8X4), rhs_scale=hs[:], start=True, stop=True)
+                                    rhs=hq.bitcast(FP8X4), rhs_scale=hs, start=True, stop=True)
                 at += n
             nc.scalar.activation(y, banks[bank][:, 0:at], ACT.Identity, bias=bias[:, c : c + 1])
 
@@ -161,7 +160,7 @@ def tile_list_modp_relu_resb_kernel(tc, tab_words, tab_scales, wu_words, wu_scal
                 nc.tensor.matmul(banks[across][:, i * P : (i + 1) * P], picked[:, i * P : (i + 1) * P], ident[:], start=(i == 0), stop=False, is_transpose=True)
             for i in range(n):
                 nc.tensor.matmul(banks[across][:, i * P : (i + 1) * P], y[:, i * P : (i + 1) * P], ident[:], start=False, stop=(i == n - 1), is_transpose=True)
-            turned = keep.tile([P, n * P], F32, name="turned%d" % span[0], align_bytes=64)
+            turned = keep.tile([P, n * P], F32, name="turned%d" % across, align_bytes=64)
             nc.scalar.copy(turned[:], banks[across][:, 0 : n * P])
             return turned
 
@@ -172,69 +171,56 @@ def tile_list_modp_relu_resb_kernel(tc, tab_words, tab_scales, wu_words, wu_scal
             nc.scalar.copy(z, banks[back][:, 0 : n * P])
 
         gather_words(0, AB, keep.tile([P, 512], U32, name="w0ab", align_bytes=64))
-        gather_words(0, C, reuse.tile([P, 512], U32, name="w0c", align_bytes=64, offset=36864))
-        gather_words(1, A, keep.tile([P, 256], U32, name="w1a", align_bytes=64))
-        gather_words(1, BC, keep.tile([P, 768], U32, name="w1bc", align_bytes=64))
-        h_t[A] = reuse.tile([P, 1024], BF16, name="hA", align_bytes=64, offset=10752)
+        gather_words(0, C, keep.tile([P, 512], U32, name="w0c", align_bytes=64))
+        gather_words(1, AB, keep.tile([P, 512], U32, name="w1ab", align_bytes=64))
+        gather_words(1, C, keep.tile([P, 512], U32, name="w1c", align_bytes=64))
+        h_t[AB] = keep.tile([P, 2048], BF16, name="hAB", align_bytes=64)
         h_t[C] = keep.tile([P, 2048], BF16, name="hC", align_bytes=64)
         for i in range(4):
             up_pass(0, i, True)
-        for i in range(2):
+        for i in range(4):
             up_pass(1, i, False)
-            relu(A, i)
-        picked_b = keep.tile([P, 256], F32, name="picked_b", align_bytes=64)
-        nc.vector.tensor_copy(picked_b[:], res[0][:].indirect(listed(B)))
-        quantise(A, 17408)
-        h_t[B] = reuse.tile([P, 1024], BF16, name="hB", align_bytes=64, offset=6144)
-        up_pass(1, 2, False)
-        relu(B, 2)
-        y0a = keep.tile([P, 256], F32, name="y0a", align_bytes=64)
-        down(0, [A], 0, y0a[:])
-        up_pass(1, 3, False)
-        relu(B, 3)
-        picked_c = reuse.tile([P, 512], F32, name="picked_c", align_bytes=64, offset=10752)
-        nc.vector.tensor_copy(picked_c[:], res[0][:].indirect(listed(C)))
-        gather_add(0, A, y0a[:])
-        quantise(B, 13312)
-        page1 = reuse.tile([P, T], F32, name="page1", align_bytes=64, offset=26624)
-        nc.gpsimd.memset(page1[:], 0.0)
-        scatter(0, A, page0)
-        y = {(c, span): keep.tile([P, span[1] - span[0]], F32, name="y%d_%d" % (c, span[0]), align_bytes=64) for c, span in ((0, B), (0, C), (1, C), (2, ALL), (3, ALL))}
+            relu(AB, i)
+        picked0 = keep.tile([P, J], F32, name="picked0", align_bytes=64)
+        nc.vector.tensor_copy(picked0[:], res[0][:].indirect(listed(ALL)))
+        quantise(AB)
+        picked1 = keep.tile([P, 768], F32, name="picked1", align_bytes=64)
+        nc.vector.tensor_copy(picked1[:], res[1][:].indirect(listed(BC)))
+        y = [keep.tile([P, J], F32, name="y%d" % c, align_bytes=64) for c in range(4)]
+        down(1, [A], 1, y[1][:, 0:256])
         for i in range(4, 8):
             up_pass(1, i, True)
             up_pass(0, i, False)
             relu(C, i)
-        quantise(C, 14336)
-        y[(1, AB)] = reuse.tile([P, 512], F32, name="y1_0", align_bytes=64, offset=36864)
-        down(1, [A, B], 1, y[(1, AB)][:])
-        down(2, [A, B], 1, y[(2, ALL)][:, 0:512])
-        down(1, [C], 5, y[(1, C)][:])
-        down(2, [C], 6, y[(2, ALL)][:, 512:1024])
-        down(0, [B], 5, y[(0, B)][:])
-        down(0, [C], 6, y[(0, C)][:])
-        z0 = keep.tile([P, 768], F32, name="z0", align_bytes=64)
-        z1 = keep.tile([P, J], F32, name="z1", align_bytes=64)
-        zs[(0, BC)] = z0
-        gather_add(1, AB, y[(1, AB)][:], z1[:, 0:512])
-        z2 = keep.tile([P, J], F32, name="z2", align_bytes=64)
-        zs[(2, ALL)] = z2
-        gather_add(2, AB, y[(2, ALL)][:, 0:512], z2[:, 0:512])
-        gather_add(1, C, y[(1, C)][:], z1[:, 512:1024])
-        gather_add(2, C, y[(2, ALL)][:, 512:1024], z2[:, 512:1024])
-        zs[(1, ALL)] = z1
-        scatter(1, ALL, page1)
-        store(1, page1)
-        turned_b = sum_across(B, picked_b[:], y[(0, B)][:], 4)
-        turned_c = sum_across(C, picked_c[:], y[(0, C)][:], 7)
-        turn_back(B, turned_b, 3, z0[:, 0:256])
-        turn_back(C, turned_c, 2, z0[:, 256:768])
-        scatter(0, BC, page0)
-        store(0, page0)
-        down(3, [A, B], 5, y[(3, ALL)][:, 0:512])
-        down(3, [C], 6, y[(3, ALL)][:, 512:1024])
-        gather_add(3, ALL, y[(3, ALL)][:])
+        gather_add(1, A, y[1][:, 0:256])
+        quantise(C)
+        page1 = reuse.tile([P, T], F32, name="page1", align_bytes=64, offset=26624)
+        nc.gpsimd.memset(page1[:], 0.0)
+        scatter(1, A, page0)
+        down(2, [AB], 2, y[2][:, 0:512])
+        down(2, [C], 3, y[2][:, 512:1024])
+        down(1, [B], 1, y[1][:, 256:512])
+        down(0, [AB], 4, y[0][:, 0:512])
+        gather_add(2, ALL, y[2][:])
         scatter(2, ALL, page1)
         store(2, page1)
+        down(1, [C], 6, y[1][:, 512:1024])
+        down(0, [C], 5, y[0][:, 512:1024])
+        down(3, [AB], 3, y[3][:, 0:512])
+        down(3, [C], 0, y[3][:, 512:1024])
+        gather_add(3, ALL, y[3][:])
+        z1 = keep.tile([P, 768], F32, name="z1", align_bytes=64)
+        z0 = keep.tile([P, J], F32, name="z0", align_bytes=64)
+        zs[(1, BC)] = z1
+        zs[(0, ALL)] = z0
+        turn_back(B, sum_across(B, picked1[:, 0:256], y[1][:, 256:512], 5), 1, z1[:, 0:256])
+        turn_back(C, sum_across(C, picked1[:, 256:768], y[1][:, 512:1024], 6), 2, z1[:, 256:768])
+        scatter(1, BC, page0)
+        store(1, page0)
+        turn_back(AB, sum_across(AB, picked0[:, 0:512], y[0][:, 0:512], 3), 4, z0[:, 0:512])
+        turn_back(C, sum_across(C, picked0[:, 512:1024], y[0][:, 512:1024], 7), 0, z0[:, 512:1024])
+        scatter(0, ALL, page1)
+        store(0, page1)
         scatter(3, ALL, page0)
         for n, queue in enumerate((nc.sync, nc.scalar)):
             queue.dma_start(out[3 * P : 4 * P, n * J : (n + 1) * J], page0[:, n * J : (n + 1) * J])

@@ -170,10 +170,9 @@ def tile_list_modp_relu_resb_kernel(tc, tab_words, tab_scales, wu_words, wu_scal
                 nc.tensor.transpose(banks[back][:, i * P : (i + 1) * P], turned[:, i * P : (i + 1) * P], ident[:])
             nc.scalar.copy(z, banks[back][:, 0 : n * P])
 
-        gather_words(0, AB, keep.tile([P, 512], U32, name="w0ab", align_bytes=64))
-        gather_words(0, C, keep.tile([P, 512], U32, name="w0c", align_bytes=64))
-        gather_words(1, AB, keep.tile([P, 512], U32, name="w1ab", align_bytes=64))
-        gather_words(1, C, keep.tile([P, 512], U32, name="w1c", align_bytes=64))
+        gather_words(0, ALL, keep.tile([P, J], U32, name="w0", align_bytes=64))
+        gather_words(1, (0, 384), keep.tile([P, 384], U32, name="w1ab", align_bytes=64))
+        gather_words(1, (384, J), keep.tile([P, 640], U32, name="w1c", align_bytes=64))
         h_t[AB] = keep.tile([P, 2048], BF16, name="hAB", align_bytes=64)
         h_t[C] = keep.tile([P, 2048], BF16, name="hC", align_bytes=64)
         for i in range(4):
@@ -202,13 +201,13 @@ def tile_list_modp_relu_resb_kernel(tc, tab_words, tab_scales, wu_words, wu_scal
         down(1, [B], 1, y[1][:, 256:512])
         down(0, [AB], 4, y[0][:, 0:512])
         gather_add(2, ALL, y[2][:])
+        down(3, [AB], 3, y[3][:, 0:512])
+        down(3, [C], 0, y[3][:, 512:1024])
+        gather_add(3, ALL, y[3][:])
         scatter(2, ALL, page1)
         store(2, page1)
         down(1, [C], 6, y[1][:, 512:1024])
         down(0, [C], 5, y[0][:, 512:1024])
-        down(3, [AB], 3, y[3][:, 0:512])
-        down(3, [C], 0, y[3][:, 512:1024])
-        gather_add(3, ALL, y[3][:])
         z1 = keep.tile([P, 768], F32, name="z1", align_bytes=64)
         z0 = keep.tile([P, J], F32, name="z0", align_bytes=64)
         zs[(1, BC)] = z1

@@ -91,13 +91,15 @@ def tile_list_modp_relu_resb_kernel(tc, tab_words, tab_scales, wu_words, wu_scal
 
         load_res(0)
         load_res(1)
-        nc.sync.dma_start(wd[:], wd_words[0].rearrange("p n i -> p (n i)").bitcast(I32))
+        wd_dram = wd_words[0].rearrange("p n i -> p (n i)").bitcast(I32)
+        nc.sync.dma_start(wd[:, P : 3 * P], wd_dram[:, P : 3 * P])
         with nc.allow_non_contiguous_dma(reason="one bias value a partition"):
             nc.sync.dma_start(bias[:], b.rearrange("(c p) -> p c", p=P))
         load_gate(A)
         load_res(2)
-        load_gate(BC)
+        nc.sync.dma_start(wd[:].rearrange("p (c n) -> p c n", c=4)[:, 0:4:3], wd_dram.rearrange("p (c n) -> p c n", c=4)[:, 0:4:3])
         load_res(3)
+        load_gate(BC)
 
         words = {}
 
@@ -157,7 +159,7 @@ def tile_list_modp_relu_resb_kernel(tc, tab_words, tab_scales, wu_words, wu_scal
         def sum_across(span, picked, y, across):
             n = (span[1] - span[0]) // P
             for i in range(n):
-                nc.tensor.matmul(banks[across][:, i * P : (i + 1) * P], picked[:, i * P : (i + 1) * P], ident[:], start=(i == 0), stop=False, is_transpose=True)
+                nc.tensor.matmul(banks[across][:, i * P : (i + 1) * P], picked[i], ident[:], start=(i == 0), stop=False, is_transpose=True)
             for i in range(n):
                 nc.tensor.matmul(banks[across][:, i * P : (i + 1) * P], y[:, i * P : (i + 1) * P], ident[:], start=False, stop=(i == n - 1), is_transpose=True)
             turned = keep.tile([P, n * P], F32, name="turned%d" % across, align_bytes=64)
@@ -174,7 +176,7 @@ def tile_list_modp_relu_resb_kernel(tc, tab_words, tab_scales, wu_words, wu_scal
         gather_words(1, (0, 384), keep.tile([P, 384], U32, name="w1ab", align_bytes=64))
         gather_words(1, (384, J), keep.tile([P, 640], U32, name="w1c", align_bytes=64))
         h_t[AB] = keep.tile([P, 2048], BF16, name="hAB", align_bytes=64)
-        h_t[C] = keep.tile([P, 2048], BF16, name="hC", align_bytes=64)
+        h_t[C] = reuse.tile([P, 2048], BF16, name="hC", align_bytes=64, offset=40960)
         for i in range(4):
             up_pass(0, i, True)
         for i in range(4):
@@ -183,41 +185,45 @@ def tile_list_modp_relu_resb_kernel(tc, tab_words, tab_scales, wu_words, wu_scal
         picked0 = keep.tile([P, J], F32, name="picked0", align_bytes=64)
         nc.vector.tensor_copy(picked0[:], res[0][:].indirect(listed(ALL)))
         quantise(AB)
-        picked1 = keep.tile([P, 768], F32, name="picked1", align_bytes=64)
-        nc.vector.tensor_copy(picked1[:], res[1][:].indirect(listed(BC)))
+        picked1 = keep.tile([P, 640], F32, name="picked1", align_bytes=64)
+        nc.vector.tensor_copy(picked1[:], res[1][:].indirect(listed((256, 896))))
         y = [keep.tile([P, J], F32, name="y%d" % c, align_bytes=64) for c in range(4)]
         down(1, [A], 1, y[1][:, 0:256])
         for i in range(4, 8):
             up_pass(1, i, True)
             up_pass(0, i, False)
             relu(C, i)
-        gather_add(1, A, y[1][:, 0:256])
         quantise(C)
+        gather_add(1, A, y[1][:, 0:256])
+        picked1_last = reuse.tile([P, 128], F32, name="picked1_last", align_bytes=64, offset=40960)
+        nc.vector.tensor_copy(picked1_last[:], res[1][:].indirect(listed((896, J))))
         page1 = reuse.tile([P, T], F32, name="page1", align_bytes=64, offset=26624)
         nc.gpsimd.memset(page1[:], 0.0)
         scatter(1, A, page0)
         down(2, [AB], 2, y[2][:, 0:512])
         down(2, [C], 3, y[2][:, 512:1024])
-        down(1, [B], 1, y[1][:, 256:512])
-        down(0, [AB], 4, y[0][:, 0:512])
         gather_add(2, ALL, y[2][:])
-        down(3, [AB], 3, y[3][:, 0:512])
+        down(3, [AB], 4, y[3][:, 0:512])
         down(3, [C], 0, y[3][:, 512:1024])
         gather_add(3, ALL, y[3][:])
+        down(1, [B], 1, y[1][:, 256:512])
+        down(0, [AB], 2, y[0][:, 0:512])
         scatter(2, ALL, page1)
         store(2, page1)
         down(1, [C], 6, y[1][:, 512:1024])
         down(0, [C], 5, y[0][:, 512:1024])
+        blocks0 = [picked0[:, j : j + P] for j in range(0, J, P)]
+        blocks1 = [picked1[:, j : j + P] for j in range(0, 640, P)] + [picked1_last[:, j : j + P] for j in range(0, 128, P)]
         z1 = keep.tile([P, 768], F32, name="z1", align_bytes=64)
         z0 = keep.tile([P, J], F32, name="z0", align_bytes=64)
         zs[(1, BC)] = z1
         zs[(0, ALL)] = z0
-        turn_back(B, sum_across(B, picked1[:, 0:256], y[1][:, 256:512], 5), 1, z1[:, 0:256])
-        turn_back(C, sum_across(C, picked1[:, 256:768], y[1][:, 512:1024], 6), 2, z1[:, 256:768])
+        turn_back(B, sum_across(B, blocks1[0:2], y[1][:, 256:512], 5), 1, z1[:, 0:256])
+        turn_back(C, sum_across(C, blocks1[2:6], y[1][:, 512:1024], 6), 2, z1[:, 256:768])
         scatter(1, BC, page0)
         store(1, page0)
-        turn_back(AB, sum_across(AB, picked0[:, 0:512], y[0][:, 0:512], 3), 4, z0[:, 0:512])
-        turn_back(C, sum_across(C, picked0[:, 512:1024], y[0][:, 512:1024], 7), 0, z0[:, 512:1024])
+        turn_back(AB, sum_across(AB, blocks0[0:4], y[0][:, 0:512], 3), 4, z0[:, 0:512])
+        turn_back(C, sum_across(C, blocks0[4:8], y[0][:, 512:1024], 7), 0, z0[:, 512:1024])
         scatter(0, ALL, page1)
         store(0, page1)
         scatter(3, ALL, page0)

@@ -172,9 +172,11 @@ def tile_list_modp_relu_resb_kernel(tc, tab_words, tab_scales, wu_words, wu_scal
                 nc.tensor.transpose(banks[back][:, i * P : (i + 1) * P], turned[:, i * P : (i + 1) * P], ident[:])
             nc.scalar.copy(z, banks[back][:, 0 : n * P])
 
-        gather_words(0, ALL, keep.tile([P, J], U32, name="w0", align_bytes=64))
-        gather_words(1, (0, 384), keep.tile([P, 384], U32, name="w1ab", align_bytes=64))
-        gather_words(1, (384, J), keep.tile([P, 640], U32, name="w1c", align_bytes=64))
+        gather_words(0, AB, keep.tile([P, 512], U32, name="w0ab", align_bytes=64))
+        gather_words(0, C, keep.tile([P, 512], U32, name="w0c", align_bytes=64))
+        gather_words(1, A, keep.tile([P, 256], U32, name="w1a", align_bytes=64))
+        gather_words(1, B, keep.tile([P, 256], U32, name="w1b", align_bytes=64))
+        gather_words(1, C, keep.tile([P, 512], U32, name="w1c", align_bytes=64))
         h_t[AB] = keep.tile([P, 2048], BF16, name="hAB", align_bytes=64)
         h_t[C] = reuse.tile([P, 2048], BF16, name="hC", align_bytes=64, offset=40960)
         for i in range(4):
@@ -197,7 +199,7 @@ def tile_list_modp_relu_resb_kernel(tc, tab_words, tab_scales, wu_words, wu_scal
         gather_add(1, A, y[1][:, 0:256])
         picked1_last = reuse.tile([P, 128], F32, name="picked1_last", align_bytes=64, offset=40960)
         nc.vector.tensor_copy(picked1_last[:], res[1][:].indirect(listed((896, J))))
-        page1 = reuse.tile([P, T], F32, name="page1", align_bytes=64, offset=26624)
+        page1 = reuse.tile([P, T], F32, name="page1", align_bytes=64, offset=43008)
         nc.gpsimd.memset(page1[:], 0.0)
         scatter(1, A, page0)
         down(2, [AB], 2, y[2][:, 0:512])

@@ -31,13 +31,15 @@ def tile_list_modp_relu_resb_kernel(tc, tab_words, tab_scales, wu_words, wu_scal
         psum = ctx.enter_context(tc.psum_pool(name="psum", bufs=1))
         banks = [psum.tile([P, 512], F32, name="bank%d" % i) for i in range(8)]
 
+        low = [keep.tile([P, T], dtype, name="low%d" % i, align_bytes=64) for i, dtype in enumerate((I32, F32, F32))]
+        high = [reuse.tile([P, T], dtype, name="high%d" % i, align_bytes=64, offset=53248 + 8192 * i) for i, dtype in enumerate((I32, F32, F32))]
         offsets = keep.tile([P, J // 16], U16, name="offsets")
         nc.sync.dma_start(offsets[:], offs)
 
         def listed(span):
             return offsets[:] if span == ALL else offsets[:, span[0] // 16 : span[1] // 16]
 
-        tabs = keep.tile([P, T], U8, name="tabs", align_bytes=64)
+        tabs = reuse.tile([P, T], U8, name="tabs", align_bytes=64, offset=51200)
         nc.vector.memset(tabs[:].bitcast(I32), 0)
         wus_raw = reuse.tile([P, 2 * R], U8, name="wus_raw", align_bytes=64, offset=26112)
         nc.vector.memset(wus_raw[:].bitcast(I32), 0)
@@ -50,8 +52,8 @@ def tile_list_modp_relu_resb_kernel(tc, tab_words, tab_scales, wu_words, wu_scal
         page0 = keep.tile([P, T], F32, name="page0", align_bytes=64)
         nc.vector.memset(page0[:], 0.0)
         wu_raw = keep.tile([P, 2, 2 * R], U8, name="wu_raw", align_bytes=64)
-        tabw = [keep.tile([P, T], I32, name="tabw%d" % a, align_bytes=64) for a in range(2)]
-        res = [keep.tile([P, T], F32, name="res%d" % c, align_bytes=64) for c in range(4)]
+        tabw = [low[0], high[0]]
+        res = [low[1], high[1], low[2], high[2]]
         gate_all = keep.tile([P, J], F32, name="gate_all", align_bytes=64)
 
         nc.sync.dma_start(wu_raw[:].bitcast(I32), wu_words.rearrange("a p w -> p a w").bitcast(I32))
@@ -97,9 +99,10 @@ def tile_list_modp_relu_resb_kernel(tc, tab_words, tab_scales, wu_words, wu_scal
             nc.sync.dma_start(bias[:], b.rearrange("(c p) -> p c", p=P))
         load_gate(A)
         load_res(2)
+        load_gate(B)
         nc.sync.dma_start(wd[:].rearrange("p (c n) -> p c n", c=4)[:, 0:4:3], wd_dram.rearrange("p (c n) -> p c n", c=4)[:, 0:4:3])
         load_res(3)
-        load_gate(BC)
+        load_gate(C)
 
         words = {}
 
@@ -202,32 +205,33 @@ def tile_list_modp_relu_resb_kernel(tc, tab_words, tab_scales, wu_words, wu_scal
         page1 = reuse.tile([P, T], F32, name="page1", align_bytes=64, offset=43008)
         nc.gpsimd.memset(page1[:], 0.0)
         scatter(1, A, page0)
+        blocks0 = [picked0[:, j : j + P] for j in range(0, J, P)]
+        blocks1 = [picked1[:, j : j + P] for j in range(0, 640, P)] + [picked1_last[:]]
         down(2, [AB], 2, y[2][:, 0:512])
         down(2, [C], 3, y[2][:, 512:1024])
         gather_add(2, ALL, y[2][:])
+        down(1, [B], 1, y[1][:, 256:512])
+        zs[(1, B)] = keep.tile([P, 256], F32, name="z1b", align_bytes=64)
+        turn_back(B, sum_across(B, blocks1[0:2], y[1][:, 256:512], 5), 6, zs[(1, B)][:])
+        scatter(1, B, page0)
         down(3, [AB], 4, y[3][:, 0:512])
         down(3, [C], 0, y[3][:, 512:1024])
         gather_add(3, ALL, y[3][:])
-        down(1, [B], 1, y[1][:, 256:512])
-        down(0, [AB], 2, y[0][:, 0:512])
+        down(1, [C], 2, y[1][:, 512:1024])
+        zs[(1, C)] = keep.tile([P, 512], F32, name="z1c", align_bytes=64)
+        turn_back(C, sum_across(C, blocks1[2:6], y[1][:, 512:1024], 3), 1, zs[(1, C)][:])
+        scatter(1, C, page0)
+        store(1, page0)
         scatter(2, ALL, page1)
         store(2, page1)
-        down(1, [C], 6, y[1][:, 512:1024])
-        down(0, [C], 5, y[0][:, 512:1024])
-        blocks0 = [picked0[:, j : j + P] for j in range(0, J, P)]
-        blocks1 = [picked1[:, j : j + P] for j in range(0, 640, P)] + [picked1_last[:, j : j + P] for j in range(0, 128, P)]
-        z1 = keep.tile([P, 768], F32, name="z1", align_bytes=64)
+        down(0, [AB], 4, y[0][:, 0:512])
+        down(0, [C], 0, y[0][:, 512:1024])
         z0 = keep.tile([P, J], F32, name="z0", align_bytes=64)
-        zs[(1, BC)] = z1
         zs[(0, ALL)] = z0
-        turn_back(B, sum_across(B, blocks1[0:2], y[1][:, 256:512], 5), 1, z1[:, 0:256])
-        turn_back(C, sum_across(C, blocks1[2:6], y[1][:, 512:1024], 6), 2, z1[:, 256:768])
-        scatter(1, BC, page0)
-        store(1, page0)
-        turn_back(AB, sum_across(AB, blocks0[0:4], y[0][:, 0:512], 3), 4, z0[:, 0:512])
-        turn_back(C, sum_across(C, blocks0[4:8], y[0][:, 512:1024], 7), 0, z0[:, 512:1024])
-        scatter(0, ALL, page1)
-        store(0, page1)
-        scatter(3, ALL, page0)
+        turn_back(AB, sum_across(AB, blocks0[0:4], y[0][:, 0:512], 7), 6, z0[:, 0:512])
+        turn_back(C, sum_across(C, blocks0[4:8], y[0][:, 512:1024], 4), 2, z0[:, 512:1024])
+        scatter(0, ALL, page0)
+        store(0, page0)
+        scatter(3, ALL, page1)
         for n, queue in enumerate((nc.sync, nc.scalar)):
-            queue.dma_start(out[3 * P : 4 * P, n * J : (n + 1) * J], page0[:, n * J : (n + 1) * J])
+            queue.dma_start(out[3 * P : 4 * P, n * J : (n + 1) * J], page1[:, n * J : (n + 1) * J])

@@ -31,15 +31,15 @@ def tile_list_modp_relu_resb_kernel(tc, tab_words, tab_scales, wu_words, wu_scal
         psum = ctx.enter_context(tc.psum_pool(name="psum", bufs=1))
         banks = [psum.tile([P, 512], F32, name="bank%d" % i) for i in range(8)]
 
-        low = [keep.tile([P, T], dtype, name="low%d" % i, align_bytes=64) for i, dtype in enumerate((I32, F32, F32))]
-        high = [reuse.tile([P, T], dtype, name="high%d" % i, align_bytes=64, offset=53248 + 8192 * i) for i, dtype in enumerate((I32, F32, F32))]
+        low = [keep.tile([P, T], dtype, name="low%d" % i, align_bytes=256) for i, dtype in enumerate((I32, F32, F32))]
+        high = [reuse.tile([P, T], dtype, name="high%d" % i, align_bytes=256, offset=53248 + 8192 * i) for i, dtype in enumerate((I32, F32, F32))]
         offsets = keep.tile([P, J // 16], U16, name="offsets")
         nc.sync.dma_start(offsets[:], offs)
 
         def listed(span):
             return offsets[:] if span == ALL else offsets[:, span[0] // 16 : span[1] // 16]
 
-        tabs = reuse.tile([P, T], U8, name="tabs", align_bytes=64, offset=51200)
+        tabs = reuse.tile([P, T], U8, name="tabs", align_bytes=256, offset=51200)
         nc.vector.memset(tabs[:].bitcast(I32), 0)
         wus_raw = reuse.tile([P, 2 * R], U8, name="wus_raw", align_bytes=64, offset=26112)
         nc.vector.memset(wus_raw[:].bitcast(I32), 0)
@@ -49,12 +49,12 @@ def tile_list_modp_relu_resb_kernel(tc, tab_words, tab_scales, wu_words, wu_scal
             nc.gpsimd.dma_start(wds[32 * q : 32 * q + 4, :].bitcast(I32), wd_scales[0, 4 * q : 4 * q + 4, :].bitcast(I32))
         bias = keep.tile([P, 4], F32, name="bias", align_bytes=64)
 
-        page0 = keep.tile([P, T], F32, name="page0", align_bytes=64)
+        page0 = keep.tile([P, T], F32, name="page0", align_bytes=256)
         nc.vector.memset(page0[:], 0.0)
-        wu_raw = keep.tile([P, 2, 2 * R], U8, name="wu_raw", align_bytes=64)
+        wu_raw = keep.tile([P, 2, 2 * R], U8, name="wu_raw", align_bytes=256)
         tabw = [low[0], high[0]]
         res = [low[1], high[1], low[2], high[2]]
-        gate_all = keep.tile([P, J], F32, name="gate_all", align_bytes=64)
+        gate_all = keep.tile([P, J], F32, name="gate_all", align_bytes=256)
 
         nc.sync.dma_start(wu_raw[:].bitcast(I32), wu_words.rearrange("a p w -> p a w").bitcast(I32))
         scale_rows = tab_scales.rearrange("a (q r) t -> r q a t", r=4)
@@ -83,7 +83,7 @@ def tile_list_modp_relu_resb_kernel(tc, tab_words, tab_scales, wu_words, wu_scal
 
         ident = reuse.tile([P, P], F32, name="ident", align_bytes=64, offset=26112)
         make_identity(nc, ident[:])
-        wd = keep.tile([P, N], I32, name="wd", align_bytes=64)
+        wd = keep.tile([P, N], I32, name="wd", align_bytes=256)
 
         def load_gate(span):
             nc.sync.dma_start(gate_all[:, span[0] : span[1]], wgo[:, span[0] : span[1]])
@@ -202,7 +202,7 @@ def tile_list_modp_relu_resb_kernel(tc, tab_words, tab_scales, wu_words, wu_scal
         gather_add(1, A, y[1][:, 0:256])
         picked1_last = reuse.tile([P, 128], F32, name="picked1_last", align_bytes=64, offset=40960)
         nc.vector.tensor_copy(picked1_last[:], res[1][:].indirect(listed((896, J))))
-        page1 = reuse.tile([P, T], F32, name="page1", align_bytes=64, offset=43008)
+        page1 = reuse.tile([P, T], F32, name="page1", align_bytes=256, offset=43008)
         nc.gpsimd.memset(page1[:], 0.0)
         scatter(1, A, page0)
         blocks0 = [picked0[:, j : j + P] for j in range(0, J, P)]

from contextlib import ExitStack

import concourse.mybir as mybir
from concourse.masks import make_identity

K, R, N, T, J = 1024, 512, 512, 2048, 1024
FLOPS = 2 * K * R * J + 2 * R * N * J

F32 = mybir.dt.float32
BF16 = mybir.dt.bfloat16
I32 = mybir.dt.int32
U32 = mybir.dt.uint32
U16 = mybir.dt.uint16
U8 = mybir.dt.uint8
FP8X4 = mybir.dt.float8_e4m3fn_x4
FP4X4 = mybir.dt.float4_e2m1fn_x4
ACT = mybir.ActivationFunctionType
MULT = mybir.AluOpType.mult
ADD = mybir.AluOpType.add

P = 128
A, B, C = (0, 256), (256, 512), (512, 1024)
AB, BC, ALL = (0, 512), (256, 1024), (0, 1024)


def tile_list_modp_relu_resb_kernel(tc, tab_words, tab_scales, wu_words, wu_scales, wd_words, wd_scales, rT, b, wgo, offs, out):
    nc = tc.nc
    with ExitStack() as ctx:
        keep = ctx.enter_context(tc.tile_pool(name="keep", bufs=1))
        reuse = ctx.enter_context(tc.tile_pool(name="reuse", bufs=1))
        psum = ctx.enter_context(tc.psum_pool(name="psum", bufs=1))
        banks = [psum.tile([P, 512], F32, name="bank%d" % i) for i in range(8)]

        low = [keep.tile([P, T], dtype, name="low%d" % i, align_bytes=256) for i, dtype in enumerate((I32, F32, F32))]
        high = [reuse.tile([P, T], dtype, name="high%d" % i, align_bytes=256, offset=53248 + 8192 * i) for i, dtype in enumerate((I32, F32, F32))]
        offsets = keep.tile([P, J // 16], U16, name="offsets")
        nc.sync.dma_start(offsets[:], offs)

        def listed(span):
            return offsets[:] if span == ALL else offsets[:, span[0] // 16 : span[1] // 16]

        tabs = reuse.tile([P, T], U8, name="tabs", align_bytes=256, offset=51200)
        nc.vector.memset(tabs[:].bitcast(I32), 0)
        wus_raw = reuse.tile([P, 2 * R], U8, name="wus_raw", align_bytes=64, offset=26112)
        nc.vector.memset(wus_raw[:].bitcast(I32), 0)
        wds = keep.tile([P, N], U8, name="wds", align_bytes=64)
        plane1 = keep.tile([P, J], U8, name="plane1", align_bytes=64)
        for q in range(4):
            nc.gpsimd.dma_start(wds[32 * q : 32 * q + 4, :].bitcast(I32), wd_scales[0, 4 * q : 4 * q + 4, :].bitcast(I32))
        bias = keep.tile([P, 4], F32, name="bias", align_bytes=64)

        page0 = keep.tile([P, T], F32, name="page0", align_bytes=256)
        nc.vector.memset(page0[:], 0.0)
        wu_raw = keep.tile([P, 2, 2 * R], U8, name="wu_raw", align_bytes=256)
        tabw = [low[0], high[0]]
        res = [low[1], high[1], low[2], high[2]]
        gate_all = keep.tile([P, J], F32, name="gate_all", align_bytes=256)

        nc.sync.dma_start(wu_raw[:].bitcast(I32), wu_words.rearrange("a p w -> p a w").bitcast(I32))
        scale_rows = tab_scales.rearrange("a (q r) t -> r q a t", r=4)
        for r in range(4):
            nc.sync.dma_start(tabs[r:P:16, :].bitcast(I32), scale_rows[r].bitcast(I32))
        nc.sync.dma_start(tabw[0][:], tab_words[0].rearrange("p t i -> p (t i)").bitcast(I32))
        for q in range(4):
            nc.sync.dma_start(wus_raw[32 * q : 32 * q + 4, :].rearrange("r (a n) -> r a n", a=2).bitcast(I32), wu_scales[:, 4 * q : 4 * q + 4, :].rearrange("a r n -> r a n").bitcast(I32))
        nc.sync.dma_start(tabw[1][:], tab_words[1].rearrange("p t i -> p (t i)").bitcast(I32))

        wu = keep.tile([P, 4 * R], U8, name="wu", align_bytes=64)
        nc.vector.tensor_copy(wu[:].bitcast(U16).rearrange("p (t g m) -> p g t m", t=4, m=8), wu_raw[:].rearrange("p a w -> p (a w)").bitcast(U16).rearrange("p (g m t) -> p g t m", t=4, m=8))

        plane0 = keep.tile([P, J], U8, name="plane0", align_bytes=64)
        nc.vector.tensor_copy(plane0[:], tabs[:].indirect(offsets[:]))
        for q in range(4):
            nc.sync.dma_start(plane1[32 * q : 32 * q + 4, :].bitcast(I32), plane0[32 * q + 16 : 32 * q + 20, :].bitcast(I32))
        planes = [plane0, plane1]

        for n in range(2):
            nc.tensor.matmul_mx(out=banks[7][:], lhsT=tabw[0][:, n * P : (n + 1) * P].bitcast(FP8X4), lhsT_scale=tabs[:, n * P : (n + 1) * P],
                                rhs=wu_raw[:, 0, :].bitcast(FP4X4), rhs_scale=wus_raw[:, 0:R], start=True, stop=True)
        wus = keep.tile([P, 2 * R], U8, name="wus", align_bytes=64)
        for a in range(2):
            nc.gpsimd.tensor_copy(wus[:].rearrange("p (t a m) -> p a t m", t=4, a=2)[:, a], wus_raw[:].rearrange("p (a m t) -> p a t m", t=4, a=2)[:, a])

        ident = reuse.tile([P, P], F32, name="ident", align_bytes=64, offset=26112)
        make_identity(nc, ident[:])
        wd = keep.tile([P, N], I32, name="wd", align_bytes=256)

        def load_gate(span):
            nc.sync.dma_start(gate_all[:, span[0] : span[1]], wgo[:, span[0] : span[1]])

        def load_res(c):
            nc.sync.dma_start(res[c][:], rT[c * P : (c + 1) * P, :])

        load_res(0)
        load_res(1)
        wd_dram = wd_words[0].rearrange("p n i -> p (n i)").bitcast(I32)
        nc.sync.dma_start(wd[:, P : 3 * P], wd_dram[:, P : 3 * P])
        with nc.allow_non_contiguous_dma(reason="one bias value a partition"):
            nc.sync.dma_start(bias[:], b.rearrange("(c p) -> p c", p=P))
        load_gate(A)
        load_res(2)
        load_gate(B)
        nc.sync.dma_start(wd[:].rearrange("p (c n) -> p c n", c=4)[:, 0:4:3], wd_dram.rearrange("p (c n) -> p c n", c=4)[:, 0:4:3])
        load_res(3)
        load_gate(C)

        words = {}

        def gather_words(a, span, tile):
            nc.vector.tensor_copy(tile[:], tabw[a][:].bitcast(U32).indirect(listed(span)))
            for j in range(span[0], span[1], P):
                words[(a, j // P)] = tile[:, j - span[0] : j - span[0] + P]

        up_bank = [banks[i] for i in (0, 1, 2, 3, 4, 5, 6, 0)]

        def up_pass(a, i, first):
            for t in range(4):
                col = t * 2 * P + a * P
                nc.tensor.matmul_mx(out=up_bank[i][:, t * P : (t + 1) * P], lhsT=wu[:, 2 * col : 2 * (col + P)].bitcast(FP4X4), lhsT_scale=wus[:, col : col + P],
                                    rhs=words[(a, i)].bitcast(FP8X4), rhs_scale=planes[a][:, i * P : (i + 1) * P], start=(first and t == 0), stop=(not first and t == 3))

        h_t = {}

        def relu(span, i):
            j = i * P - span[0]
            nc.scalar.activation(h_t[span][:, 4 * j : 4 * (j + P)].rearrange("p (j t) -> p j t", t=4), up_bank[i][:].rearrange("p (t j) -> p j t", t=4), ACT.Relu)

        coded = {}

        def quantise(span):
            n = span[1] - span[0]
            hq = keep.tile([P, n], U32, name="hq%d" % span[0], align_bytes=64)
            hs = keep.tile([P, n], U8, name="hs%d" % span[0], align_bytes=64)
            nc.vector.quantize_mx(out=hq[:].bitcast(FP8X4), scales=hs[:], in_=h_t[span][:])
            coded[span] = (hq, hs)

        def down(c, spans, bank, y):
            at = 0
            for span in spans:
                half = AB if span[1] <= AB[1] else C
                hq, hs = (t[:, span[0] - half[0] : span[1] - half[0]] for t in coded[half])
                n = span[1] - span[0]
                nc.tensor.matmul_mx(out=banks[bank][:, at : at + n], lhsT=wd[:, c * P : (c + 1) * P].bitcast(FP8X4), lhsT_scale=wds[:, c * P : (c + 1) * P],
                                    rhs=hq.bitcast(FP8X4), rhs_scale=hs, start=True, stop=True)
                at += n
            nc.scalar.activation(y, banks[bank][:, 0:at], ACT.Identity, bias=bias[:, c : c + 1])

        zs = {}

        def gather_add(c, span, y, z=None):
            if z is None:
                z = keep.tile([P, span[1] - span[0]], F32, name="z%d_%d" % (c, span[0]), align_bytes=64)[:]
            nc.vector.tensor_tensor(z, res[c][:].indirect(listed(span)), y, ADD)
            zs[(c, span)] = z

        def scatter(c, span, page):
            nc.vector.tensor_tensor(page[:].indirect(listed(span)), zs[(c, span)][:], gate_all[:, span[0] : span[1]], MULT)

        def store(c, page):
            nc.sync.dma_start(out[c * P : (c + 1) * P, :], page[:])

        def sum_across(span, picked, y, across):
            n = (span[1] - span[0]) // P
            for i in range(n):
                nc.tensor.matmul(banks[across][:, i * P : (i + 1) * P], picked[i], ident[:], start=(i == 0), stop=False, is_transpose=True)
            for i in range(n):
                nc.tensor.matmul(banks[across][:, i * P : (i + 1) * P], y[:, i * P : (i + 1) * P], ident[:], start=False, stop=(i == n - 1), is_transpose=True)
            turned = keep.tile([P, n * P], F32, name="turned%d" % across, align_bytes=64)
            nc.scalar.copy(turned[:], banks[across][:, 0 : n * P])
            return turned

        def turn_back(span, turned, back, z):
            n = (span[1] - span[0]) // P
            for i in range(n):
                nc.tensor.transpose(banks[back][:, i * P : (i + 1) * P], turned[:, i * P : (i + 1) * P], ident[:])
            nc.scalar.copy(z, banks[back][:, 0 : n * P])

        gather_words(0, AB, keep.tile([P, 512], U32, name="w0ab", align_bytes=64))
        gather_words(0, C, keep.tile([P, 512], U32, name="w0c", align_bytes=64))
        gather_words(1, A, keep.tile([P, 256], U32, name="w1a", align_bytes=64))
        gather_words(1, B, keep.tile([P, 256], U32, name="w1b", align_bytes=64))
        gather_words(1, C, keep.tile([P, 512], U32, name="w1c", align_bytes=64))
        h_t[AB] = keep.tile([P, 2048], BF16, name="hAB", align_bytes=64)
        h_t[C] = reuse.tile([P, 2048], BF16, name="hC", align_bytes=64, offset=40960)
        for i in range(4):
            up_pass(0, i, True)
        for i in range(4):
            up_pass(1, i, False)
            relu(AB, i)
        picked0 = keep.tile([P, J], F32, name="picked0", align_bytes=64)
        nc.vector.tensor_copy(picked0[:], res[0][:].indirect(listed(ALL)))
        quantise(AB)
        picked1 = keep.tile([P, 640], F32, name="picked1", align_bytes=64)
        nc.vector.tensor_copy(picked1[:], res[1][:].indirect(listed((256, 896))))
        y = [keep.tile([P, J], F32, name="y%d" % c, align_bytes=64) for c in range(4)]
        down(1, [A], 1, y[1][:, 0:256])
        for i in range(4, 8):
            up_pass(1, i, True)
            up_pass(0, i, False)
            relu(C, i)
        quantise(C)
        gather_add(1, A, y[1][:, 0:256])
        picked1_last = reuse.tile([P, 128], F32, name="picked1_last", align_bytes=64, offset=40960)
        nc.vector.tensor_copy(picked1_last[:], res[1][:].indirect(listed((896, J))))
        page1 = reuse.tile([P, T], F32, name="page1", align_bytes=256, offset=43008)
        nc.gpsimd.memset(page1[:], 0.0)
        scatter(1, A, page0)
        blocks0 = [picked0[:, j : j + P] for j in range(0, J, P)]
        blocks1 = [picked1[:, j : j + P] for j in range(0, 640, P)] + [picked1_last[:]]
        down(2, [AB], 2, y[2][:, 0:512])
        down(2, [C], 3, y[2][:, 512:1024])
        gather_add(2, ALL, y[2][:])
        down(1, [B], 1, y[1][:, 256:512])
        zs[(1, B)] = keep.tile([P, 256], F32, name="z1b", align_bytes=64)
        turn_back(B, sum_across(B, blocks1[0:2], y[1][:, 256:512], 5), 6, zs[(1, B)][:])
        scatter(1, B, page0)
        down(3, [AB], 4, y[3][:, 0:512])
        down(3, [C], 0, y[3][:, 512:1024])
        gather_add(3, ALL, y[3][:])
        down(1, [C], 2, y[1][:, 512:1024])
        zs[(1, C)] = keep.tile([P, 512], F32, name="z1c", align_bytes=64)
        turn_back(C, sum_across(C, blocks1[2:6], y[1][:, 512:1024], 3), 1, zs[(1, C)][:])
        scatter(1, C, page0)
        store(1, page0)
        scatter(2, ALL, page1)
        store(2, page1)
        down(0, [AB], 4, y[0][:, 0:512])
        down(0, [C], 0, y[0][:, 512:1024])
        z0 = keep.tile([P, J], F32, name="z0", align_bytes=64)
        zs[(0, ALL)] = z0
        turn_back(AB, sum_across(AB, blocks0[0:4], y[0][:, 0:512], 7), 6, z0[:, 0:512])
        turn_back(C, sum_across(C, blocks0[4:8], y[0][:, 512:1024], 4), 2, z0[:, 512:1024])
        scatter(0, ALL, page0)
        store(0, page0)
        scatter(3, ALL, page1)
        for n, queue in enumerate((nc.sync, nc.scalar)):
            queue.dma_start(out[3 * P : 4 * P, n * J : (n + 1) * J], page1[:, n * J : (n + 1) * J])
